import numpy as np
import ml_dtypes


def mxq(x, axis, fmt="e4m3"):
    dtype, down = {"e4m3": (ml_dtypes.float8_e4m3fn, 7), "e5m2": (ml_dtypes.float8_e5m2, 14)}[fmt]
    v = np.moveaxis(np.asarray(x, np.float32).astype(ml_dtypes.bfloat16).astype(np.float64), axis, -1)
    blocks = v.reshape(v.shape[:-1] + (-1, 32))
    amax = np.abs(blocks).max(-1, keepdims=True)
    byte = np.maximum(np.where(amax > 0, np.frexp(amax)[1] - 1 + 127, 0) - down, 1)
    scale = np.exp2(byte - 127.0)
    codes = (blocks / scale).astype(np.float32).astype(dtype).astype(np.float64)
    return np.moveaxis((codes * scale).reshape(v.shape), -1, axis)


WIDE = False


def mx_kscale(k):
    if not WIDE:
        return np.ones(k)
    levels = np.array([24, -24, 12, -12, 0])
    if k % 512:
        return np.exp2(np.random.permutation(np.resize(levels, k // 32))).repeat(32)
    a = np.empty((k // 512, 16))
    for p in range(k // 512):
        a[p, :8] = np.random.permutation(np.resize(levels, 8))
        for g in range(8):
            far = levels[np.abs(levels - a[p, g]) >= 10]
            a[p, g + 8] = far[np.random.randint(len(far))]
    return np.exp2(a.ravel()).repeat(32)


def f64(x):
    return np.asarray(x).astype(np.float64)


def striped(idx):
    return np.tile(idx.reshape(-1, 16).T, (8, 1)).astype(np.uint16)


def unstriped(offs):
    return offs[:16].T.reshape(-1).astype(np.int64)


E2M1 = np.array([0.0, 0.5, 1.0, 1.5, 2.0, 3.0, 4.0, 6.0, -0.0, -0.5, -1.0, -1.5, -2.0, -3.0, -4.0, -6.0])


def pack_weight(w, fmt):
    k, n = w.shape
    w = f64(np.asarray(w, np.float32).astype(ml_dtypes.bfloat16)).reshape(k // 32, 32, n)
    amax = np.abs(w).max(1)
    if fmt == "e4m3":
        byte = np.frexp(amax)[1] - 1 + 127 - 7
    else:
        mant, ex = np.frexp(amax / 6.0)
        byte = np.where(mant > 0.5, ex, ex - 1) + 127
    byte = np.clip(np.where(amax > 0, byte, 1), 1, 254)
    scaled = (w * np.exp2(127.0 - byte)[:, None, :]).reshape(k, n).astype(np.float32)
    by_word = np.ascontiguousarray(scaled.reshape(k // 512, 128, 4, n).transpose(0, 1, 3, 2))
    if fmt == "e4m3":
        words = by_word.astype(ml_dtypes.float8_e4m3fn).view(np.uint8)
    else:
        c = by_word.astype(ml_dtypes.float4_e2m1fn).view(np.uint8) & 0xF
        words = (c[..., 0::2] | (c[..., 1::2] << 4)).reshape(k // 512, 128, 2 * n)
    return np.ascontiguousarray(words), np.ascontiguousarray(byte.astype(np.uint8).reshape(k // 512, 16, n))


def unpack_weight(words, scales, fmt):
    g, _, n = scales.shape
    words = np.ascontiguousarray(words).reshape(g, 128, n, -1)
    if fmt == "e4m3":
        vals = words.view(ml_dtypes.float8_e4m3fn).astype(np.float64)
    else:
        nib = np.empty((g, 128, n, 4), np.uint8)
        nib[..., 0::2] = words & 0xF
        nib[..., 1::2] = words >> 4
        vals = E2M1[nib]
    vals = vals * np.repeat(np.exp2(scales.astype(np.float64) - 127.0), 8, axis=1)[..., None]
    return vals.transpose(0, 1, 3, 2).reshape(g * 512, n)


def pack_table4(v):
    words, scales = pack_weight(v, "e2m1")
    g, t = words.shape[0] // 2, v.shape[1]
    return np.ascontiguousarray(words.reshape(g, 2, 128, t, 2).transpose(0, 2, 3, 1, 4).reshape(g, 128, t, 4)), scales


def unpack_table4(words, scales):
    g, _, t, _ = words.shape
    return unpack_weight(words.reshape(g, 128, t, 2, 2).transpose(0, 3, 1, 2, 4).reshape(2 * g, 128, 2 * t), scales, "e2m1")


def silu(f):
    return f / (1.0 + np.exp(-np.maximum(f, -700.0)))


K, R, N, T, J = 1024, 512, 256, 2048, 1024


def setup_inputs():
    n = np.random.standard_normal
    s = mx_kscale(K)[:, None]
    u = mx_kscale(R)[:, None]
    p_tab = pack_table4(n((K, T)) * s)
    p_w0 = pack_weight(n((K, R)) / np.sqrt(3 * K) / s, "e4m3")
    p_w1 = pack_weight(n((K, R)) / np.sqrt(3 * K) / s, "e4m3")
    p_w2 = pack_weight(n((K, R)) / np.sqrt(3 * K) / s, "e4m3")
    p_wd = pack_weight(n((R, N)) / np.sqrt(R) / u, "e2m1")
    return {
        "tab_words": p_tab[0],
        "tab_scales": p_tab[1],
        "w0_words": p_w0[0],
        "w0_scales": p_w0[1],
        "w1_words": p_w1[0],
        "w1_scales": p_w1[1],
        "w2_words": p_w2[0],
        "w2_scales": p_w2[1],
        "sm": (np.random.uniform(0.5, 2.0, R) * u[:, 0]).astype(np.float32),
        "wd_words": p_wd[0],
        "wd_scales": p_wd[1],
        "res": (n((N, J))).astype(np.float32),
        "offs": striped(np.concatenate([np.random.permutation(T)[:J] for _ in range(3)])),
    }


def reference(tab_words, tab_scales, w0_words, w0_scales, w1_words, w1_scales, w2_words, w2_scales, sm, wd_words, wd_scales, res, offs):
    idx = unstriped(offs).reshape(3, J)
    tab_ = unpack_table4(tab_words, tab_scales)[:, idx]
    w0_ = unpack_weight(w0_words, w0_scales, "e4m3")
    w1_ = unpack_weight(w1_words, w1_scales, "e4m3")
    w2_ = unpack_weight(w2_words, w2_scales, "e4m3")
    a = w0_.T @ tab_[:, 0] + w1_.T @ tab_[:, 1] + w2_.T @ tab_[:, 2]
    h = f64(sm)[:, None] * silu(a)
    h_ = mxq(h, 0, "e4m3")
    wd_ = unpack_weight(wd_words, wd_scales, "e2m1")
    y = wd_.T @ h_
    return f64(res) + y

@@ -1,0 +1,214 @@
+from contextlib import ExitStack
+
+import concourse.mybir as mybir
+from concourse.masks import make_identity
+
+K, R, N, T, J = 1024, 512, 256, 2048, 1024
+FLOPS = 2 * (3 * K * R * J + R * N * J)
+
+F32 = mybir.dt.float32
+BF16 = mybir.dt.bfloat16
+I32 = mybir.dt.int32
+U32 = mybir.dt.uint32
+U16 = mybir.dt.uint16
+U8 = mybir.dt.uint8
+FP8X4 = mybir.dt.float8_e4m3fn_x4
+FP4X4 = mybir.dt.float4_e2m1fn_x4
+ACT = mybir.ActivationFunctionType
+ALU = mybir.AluOpType
+
+P = 128
+LISTS = 3
+BLOCK = 256
+TILES = BLOCK // P
+BLOCKS = J // BLOCK
+STEPS = LISTS * BLOCKS
+LEAD = 3
+
+
+def tile_list_rvq_silu_res_kernel(
+    tc, tab_words, tab_scales, w0_words, w0_scales, w1_words, w1_scales, w2_words, w2_scales,
+    sm, wd_words, wd_scales, res, offs, out,
+):
+    nc = tc.nc
+    w_words = (w0_words, w1_words, w2_words)
+    w_scales = (w0_scales, w1_scales, w2_scales)
+    res_v = res.rearrange("(h p) j -> p h j", p=P)
+    out_v = out.rearrange("(h p) j -> p h j", p=P)
+
+    with ExitStack() as ctx:
+        keep = ctx.enter_context(tc.tile_pool(name="keep", bufs=1))
+        ring = ctx.enter_context(tc.tile_pool(name="ring", bufs=STEPS))
+        psum = ctx.enter_context(tc.psum_pool(name="psum", bufs=1))
+
+        offsets = keep.tile([P, LISTS * J // 16], U16, name="offsets")
+        nc.sync.dma_start(offsets[:], offs)
+
+        tab_s = keep.tile([P, T // 4], I32, name="tab_s", align_bytes=64)
+        nc.gpsimd.memset(tab_s[:], 0)
+        sm_sb = keep.tile([P, 4], F32, name="sm_sb")
+        nc.sync.dma_start(sm_sb[:], sm.rearrange("(p t) -> p t", t=4))
+        ts = tab_scales.bitcast(I32)
+        for q in range(4):
+            queue = (nc.sync, nc.scalar)[q % 2]
+            queue.dma_start(tab_s[32 * q : 32 * q + 8, :], ts[:, 4 * q : 4 * q + 4, :])
+        tab_w = keep.tile([P, T], I32, name="tab_w", align_bytes=64)
+        nc.sync.dma_start(tab_w[:], tab_words[0].rearrange("p n t -> p (n t)").bitcast(I32))
+
+        planes = keep.tile([P, (2 * LISTS * R + N) // 4], I32, name="planes", align_bytes=64)
+        nc.vector.memset(planes[:], 0)
+        moved_all = keep.tile([P, LISTS * J // 4], I32, name="moved_all", align_bytes=64)
+        nc.vector.memset(moved_all[96:128, :], 0)
+        ident = keep.tile([P, P], F32, name="ident", align_bytes=64)
+        make_identity(nc, ident[:])
+
+        w_sb = [keep.tile([P, 2, R], I32, name="w%d" % g, align_bytes=64) for g in range(LISTS)]
+        w_plane = [planes[:, g * 256 : (g + 1) * 256].rearrange("p (a n) -> p a n", a=2) for g in range(LISTS)]
+
+        def load_weight(g):
+            src = w_scales[g].bitcast(I32)
+            for q in range(4):
+                nc.scalar.dma_start(w_plane[g][32 * q : 32 * q + 4, :, :], src[:, 4 * q : 4 * q + 4, :].rearrange("a r n -> r a n"))
+            nc.sync.dma_start(w_sb[g][:], w_words[g].rearrange("a p n t -> p a (n t)").bitcast(I32))
+
+        wd_plane = planes[:, LISTS * 256 : LISTS * 256 + N // 4]
+        wd_sb = keep.tile([P, 2 * N // 4], I32, name="wd_sb", align_bytes=64)
+        res_sb = keep.tile([P, 2, J], F32, name="res_sb")
+
+        def load_rest():
+            nc.sync.dma_start(wd_sb[:], wd_words[0].bitcast(I32))
+            for q in range(4):
+                nc.sync.dma_start(wd_plane[32 * q : 32 * q + 4, :], wd_scales.bitcast(I32)[0, 4 * q : 4 * q + 4, :])
+            nc.sync.dma_start(res_sb[:], res_v)
+
+        picked = {}
+        span = LISTS * BLOCK // 4
+        moved = [moved_all[:, b * span : (b + 1) * span].bitcast(U8).rearrange("p (g n) -> p g n", g=LISTS) for b in range(BLOCKS)]
+
+        def list_slice(step):
+            b, g = divmod(step, LISTS)
+            first = (g * J + b * BLOCK) // 16
+            return offsets[:, first : first + BLOCK // 16]
+
+        def gather_scales(step):
+            b, g = divmod(step, LISTS)
+            if g == 0:
+                picked[b] = keep.tile([P, LISTS, BLOCK], U8, name="picked", tag="gate%d" % b, align_bytes=64)
+            nc.vector.tensor_copy(picked[b][:, g, :], tab_s[:].bitcast(U8).indirect(list_slice(step)))
+            if g == LISTS - 1:
+                src = picked[b][:].rearrange("p g n -> p (g n)").bitcast(I32)
+                dst = moved_all[:, b * span : (b + 1) * span]
+                queue = nc.scalar if b < 2 else nc.sync
+                queue.dma_start(dst[0:112, :], src[4:116, :])
+
+        def gather_words(step):
+            if step == 0:
+                words = keep.tile([P, BLOCK], U32, name="words", tag="gate1", align_bytes=64)
+            else:
+                words = ring.tile([P, BLOCK], U32, name="words", bufs=2, align_bytes=64)
+            nc.vector.tensor_copy(words[:], tab_w[:].bitcast(U32).indirect(list_slice(step)))
+            return words
+
+        def part(step, words):
+            if step in (1, 4):
+                parted = keep.tile([P, 2, 2 * BLOCK], U8, name="parted", tag="gate%d" % (step // LISTS + 2), align_bytes=64)
+            else:
+                parted = ring.tile([P, 2, 2 * BLOCK], U8, name="parted", bufs=3, align_bytes=64)
+            nc.vector.tensor_copy(parted[:].bitcast(U16), words[:].bitcast(U16).rearrange("p (n d) -> p d n", d=2))
+            return parted
+
+        acc = {}
+
+        def project(step, parted):
+            b, g = divmod(step, LISTS)
+            if g == 0:
+                for i in range(TILES):
+                    acc[b, i] = psum.tile([P, R], F32, name="acc", bufs=4)
+            if step == STEPS - 1:
+                order = [(a, i) for i in range(TILES) for a in range(2)]
+            else:
+                order = [(a, i) for a in range(2) for i in range(TILES)]
+            for a, i in order:
+                plane = (picked[b][:], moved[b])[a]
+                nc.tensor.matmul_mx(
+                    out=acc[b, i][:],
+                    lhsT=parted[:, a, 2 * P * i : 2 * P * (i + 1)].bitcast(FP4X4),
+                    lhsT_scale=plane[:, g, P * i : P * (i + 1)],
+                    rhs=w_sb[g][:, a, :].bitcast(FP8X4),
+                    rhs_scale=w_plane[g][:, a, :].bitcast(U8),
+                    start=(g == 0 and a == 0),
+                    stop=(g == LISTS - 1 and a == 1),
+                )
+
+        def activate(b, i):
+            act = ring.tile([P, 4, P], F32, name="act", align_bytes=64)
+            nc.scalar.activation(act[:], acc[b, i][:].rearrange("j (m t) -> j t m", t=4), ACT.Silu)
+            turned = psum.tile([P, 4, P], F32, name="turned", bufs=2)
+            for t in range(4):
+                nc.tensor.transpose(turned[:, t, :], act[:, t, :], ident[:])
+            return turned
+
+        def smooth_scalar(turned, h_cols):
+            rows = ring.tile([P, 4, P], BF16, name="rows", align_bytes=64)
+            for t in range(4):
+                nc.scalar.activation(rows[:, t, :], turned[:, t, :], ACT.Copy, scale=sm_sb[:, t : t + 1])
+            nc.scalar.copy(h_cols, rows[:].rearrange("p t j -> p j t"))
+
+        def smooth_vector(turned, h_cols):
+            nc.vector.tensor_tensor(h_cols, turned[:].rearrange("p t j -> p j t"),
+                                    sm_sb[:].unsqueeze(1).to_broadcast([P, P, 4]), ALU.mult)
+
+        def finish(h, first, width):
+            codes = ring.tile([P, width], U32, name="codes", align_bytes=64)
+            scales = ring.tile([P, width], U8, name="scales", align_bytes=64)
+            nc.vector.quantize_mx(out=codes[:].bitcast(FP8X4), scales=scales[:], in_=h.rearrange("p j t -> p (j t)"))
+            y = psum.tile([P, 2, width], F32, name="y", bufs=2)
+            for half in range(2):
+                nc.tensor.matmul_mx(
+                    out=y[:, half, :],
+                    lhsT=wd_sb[:].bitcast(U8)[:, 2 * P * half : 2 * P * (half + 1)].bitcast(FP4X4),
+                    lhsT_scale=wd_plane.bitcast(U8)[:, P * half : P * (half + 1)],
+                    rhs=codes[:].bitcast(FP8X4),
+                    rhs_scale=scales[:],
+                    start=True,
+                    stop=True,
+                )
+            result = ring.tile([P, 2, width], F32, name="result")
+            nc.vector.tensor_tensor(result[:], y[:], res_sb[:, :, first : first + width], ALU.add)
+            nc.sync.dma_start(out_v[:, :, first : first + width], result[:])
+
+        load_weight(0)
+        for step in range(LEAD):
+            gather_scales(step)
+        load_weight(1)
+        load_weight(2)
+        load_rest()
+        hs = {}
+        for step in range(STEPS):
+            b, g = divmod(step, LISTS)
+            words = gather_words(step)
+            if step == 1:
+                gather_scales(LEAD)
+                parted = part(step, words)
+                gather_scales(step + LEAD)
+            else:
+                if 0 < step < STEPS - LEAD:
+                    gather_scales(step + LEAD)
+                parted = part(step, words)
+            project(step, parted)
+            if b > 0 and g == 0:
+                hs[b - 1] = ring.tile([P, BLOCK, 4], BF16, name="h", align_bytes=64)
+                turned = [activate(b - 1, i) for i in range(TILES)]
+                for i in range(TILES):
+                    smooth_scalar(turned[i], hs[b - 1][:, P * i : P * (i + 1), :])
+            if b == BLOCKS - 1 and g < LISTS - 1:
+                finish(hs[g][:], g * BLOCK, BLOCK)
+        last = BLOCKS - 1
+        turned = [activate(last, i) for i in range(TILES)]
+        for b in range(last - 1, last):
+            finish(hs[b][:], b * BLOCK, BLOCK)
+        h = ring.tile([P, BLOCK, 4], BF16, name="h", align_bytes=64)
+        for i in range(TILES):
+            smooth_vector(turned[i], h[:, P * i : P * (i + 1), :])
+        for i in range(TILES):
+            finish(h[:, P * i : P * (i + 1), :], last * BLOCK + P * i, P)

@@ -23,7 +23,7 @@ BLOCK = 256
 TILES = BLOCK // P
 BLOCKS = J // BLOCK
 STEPS = LISTS * BLOCKS
-LEAD = 3
+GROUP = 4
 
 
 def tile_list_rvq_silu_res_kernel(
@@ -45,45 +45,44 @@ def tile_list_rvq_silu_res_kernel(
         nc.sync.dma_start(offsets[:], offs)
 
         tab_s = keep.tile([P, T // 4], I32, name="tab_s", align_bytes=64)
-        nc.gpsimd.memset(tab_s[:], 0)
+        nc.vector.memset(tab_s[:], 0)
         sm_sb = keep.tile([P, 4], F32, name="sm_sb")
         nc.sync.dma_start(sm_sb[:], sm.rearrange("(p t) -> p t", t=4))
         ts = tab_scales.bitcast(I32)
         for q in range(4):
-            queue = (nc.sync, nc.scalar)[q % 2]
-            queue.dma_start(tab_s[32 * q : 32 * q + 8, :], ts[:, 4 * q : 4 * q + 4, :])
+            nc.sync.dma_start(tab_s[32 * q : 32 * q + 8, :], ts[:, 4 * q : 4 * q + 4, :])
         tab_w = keep.tile([P, T], I32, name="tab_w", align_bytes=64)
         nc.sync.dma_start(tab_w[:], tab_words[0].rearrange("p n t -> p (n t)").bitcast(I32))
 
         planes = keep.tile([P, (2 * LISTS * R + N) // 4], I32, name="planes", align_bytes=64)
-        nc.vector.memset(planes[:], 0)
+        nc.gpsimd.memset(planes[:, 256:512], 0)
+        nc.vector.memset(planes[:, 0:256], 0)
+        nc.vector.memset(planes[:, 512:], 0)
         moved_all = keep.tile([P, LISTS * J // 4], I32, name="moved_all", align_bytes=64)
         nc.vector.memset(moved_all[96:128, :], 0)
         ident = keep.tile([P, P], F32, name="ident", align_bytes=64)
-        make_identity(nc, ident[:])
 
         w_sb = [keep.tile([P, 2, R], I32, name="w%d" % g, align_bytes=64) for g in range(LISTS)]
         w_plane = [planes[:, g * 256 : (g + 1) * 256].rearrange("p (a n) -> p a n", a=2) for g in range(LISTS)]
 
         def load_weight(g):
+            nc.sync.dma_start(w_sb[g][:], w_words[g].rearrange("a p n t -> p a (n t)").bitcast(I32))
             src = w_scales[g].bitcast(I32)
             for q in range(4):
-                nc.scalar.dma_start(w_plane[g][32 * q : 32 * q + 4, :, :], src[:, 4 * q : 4 * q + 4, :].rearrange("a r n -> r a n"))
-            nc.sync.dma_start(w_sb[g][:], w_words[g].rearrange("a p n t -> p a (n t)").bitcast(I32))
+                (nc.gpsimd if g == 1 else nc.sync).dma_start(
+                    w_plane[g][32 * q : 32 * q + 4, :, :], src[:, 4 * q : 4 * q + 4, :].rearrange("a r n -> r a n"))
 
         wd_plane = planes[:, LISTS * 256 : LISTS * 256 + N // 4]
         wd_sb = keep.tile([P, 2 * N // 4], I32, name="wd_sb", align_bytes=64)
-        res_sb = keep.tile([P, 2, J], F32, name="res_sb")
 
         def load_rest():
             nc.sync.dma_start(wd_sb[:], wd_words[0].bitcast(I32))
             for q in range(4):
                 nc.sync.dma_start(wd_plane[32 * q : 32 * q + 4, :], wd_scales.bitcast(I32)[0, 4 * q : 4 * q + 4, :])
-            nc.sync.dma_start(res_sb[:], res_v)
 
         picked = {}
-        span = LISTS * BLOCK // 4
-        moved = [moved_all[:, b * span : (b + 1) * span].bitcast(U8).rearrange("p (g n) -> p g n", g=LISTS) for b in range(BLOCKS)]
+        span = GROUP * BLOCK // 4
+        moved = moved_all[:].bitcast(U8).rearrange("p (s n) -> p s n", s=STEPS)
 
         def list_slice(step):
             b, g = divmod(step, LISTS)
@@ -91,14 +90,14 @@ def tile_list_rvq_silu_res_kernel(
             return offsets[:, first : first + BLOCK // 16]
 
         def gather_scales(step):
-            b, g = divmod(step, LISTS)
-            if g == 0:
-                picked[b] = keep.tile([P, LISTS, BLOCK], U8, name="picked", tag="gate%d" % b, align_bytes=64)
-            nc.vector.tensor_copy(picked[b][:, g, :], tab_s[:].bitcast(U8).indirect(list_slice(step)))
-            if g == LISTS - 1:
-                src = picked[b][:].rearrange("p g n -> p (g n)").bitcast(I32)
-                dst = moved_all[:, b * span : (b + 1) * span]
-                queue = nc.scalar if b < 2 else nc.sync
+            c, s = divmod(step, GROUP)
+            if s == 0:
+                picked[c] = keep.tile([P, GROUP, BLOCK], U8, name="picked", tag="gate%d" % c, align_bytes=64)
+            nc.vector.tensor_copy(picked[c][:, s, :], tab_s[:].bitcast(U8).indirect(list_slice(step)))
+            if s == GROUP - 1:
+                src = picked[c][:].rearrange("p g n -> p (g n)").bitcast(I32)
+                dst = moved_all[:, c * span : (c + 1) * span]
+                queue = nc.scalar if c == 0 else nc.sync
                 queue.dma_start(dst[0:112, :], src[4:116, :])
 
         def gather_words(step):
@@ -110,8 +109,8 @@ def tile_list_rvq_silu_res_kernel(
             return words
 
         def part(step, words):
-            if step in (1, 4):
-                parted = keep.tile([P, 2, 2 * BLOCK], U8, name="parted", tag="gate%d" % (step // LISTS + 2), align_bytes=64)
+            if step in (2, 3):
+                parted = keep.tile([P, 2, 2 * BLOCK], U8, name="parted", tag="gate%d" % step, align_bytes=64)
             else:
                 parted = ring.tile([P, 2, 2 * BLOCK], U8, name="parted", bufs=3, align_bytes=64)
             nc.vector.tensor_copy(parted[:].bitcast(U16), words[:].bitcast(U16).rearrange("p (n d) -> p d n", d=2))
@@ -129,11 +128,11 @@ def tile_list_rvq_silu_res_kernel(
             else:
                 order = [(a, i) for a in range(2) for i in range(TILES)]
             for a, i in order:
-                plane = (picked[b][:], moved[b])[a]
+                plane = (picked[step // GROUP][:, step % GROUP, :], moved[:, step, :])[a]
                 nc.tensor.matmul_mx(
                     out=acc[b, i][:],
                     lhsT=parted[:, a, 2 * P * i : 2 * P * (i + 1)].bitcast(FP4X4),
-                    lhsT_scale=plane[:, g, P * i : P * (i + 1)],
+                    lhsT_scale=plane[:, P * i : P * (i + 1)],
                     rhs=w_sb[g][:, a, :].bitcast(FP8X4),
                     rhs_scale=w_plane[g][:, a, :].bitcast(U8),
                     start=(g == 0 and a == 0),
@@ -178,24 +177,28 @@ def tile_list_rvq_silu_res_kernel(
             nc.sync.dma_start(out_v[:, :, first : first + width], result[:])
 
         load_weight(0)
-        for step in range(LEAD):
-            gather_scales(step)
         load_weight(1)
+        for step in range(GROUP):
+            gather_scales(step)
         load_weight(2)
+        make_identity(nc, ident[:])
         load_rest()
         hs = {}
+        before = {3: (6,)}
+        after = {1: (4,), 2: (5,), 3: (7,), 4: (8,), 5: (9, 10), 6: (11,)}
+        words = gather_words(0)
         for step in range(STEPS):
             b, g = divmod(step, LISTS)
-            words = gather_words(step)
-            if step == 1:
-                gather_scales(LEAD)
-                parted = part(step, words)
-                gather_scales(step + LEAD)
-            else:
-                if 0 < step < STEPS - LEAD:
-                    gather_scales(step + LEAD)
-                parted = part(step, words)
-            project(step, parted)
+            ahead = gather_words(step + 1) if step + 1 < STEPS else None
+            for s in before.get(step, ()):
+                gather_scales(s)
+            project(step, part(step, words))
+            words = ahead
+            for s in after.get(step, ()):
+                gather_scales(s)
+            if step == 3:
+                res_sb = keep.tile([P, 2, J], F32, name="res_sb", tag="gate3", align_bytes=64)
+                nc.sync.dma_start(res_sb[:], res_v)
             if b > 0 and g == 0:
                 hs[b - 1] = ring.tile([P, BLOCK, 4], BF16, name="h", align_bytes=64)
                 turned = [activate(b - 1, i) for i in range(TILES)]

@@ -39,6 +39,7 @@ def tile_list_rvq_silu_res_kernel(
     with ExitStack() as ctx:
         keep = ctx.enter_context(tc.tile_pool(name="keep", bufs=1))
         ring = ctx.enter_context(tc.tile_pool(name="ring", bufs=STEPS))
+        shared = ctx.enter_context(tc.tile_pool(name="shared", bufs=1))
         psum = ctx.enter_context(tc.psum_pool(name="psum", bufs=1))
 
         offsets = keep.tile([P, LISTS * J // 16], U16, name="offsets")
@@ -92,7 +93,7 @@ def tile_list_rvq_silu_res_kernel(
         def gather_scales(step):
             c, s = divmod(step, GROUP)
             if s == 0:
-                picked[c] = keep.tile([P, GROUP, BLOCK], U8, name="picked", tag="gate%d" % c, align_bytes=64)
+                picked[c] = shared.tile([P, GROUP, BLOCK], U8, name="picked%d" % c, offset=(7168, 1024, 6144)[c], align_bytes=64)
             nc.vector.tensor_copy(picked[c][:, s, :], tab_s[:].bitcast(U8).indirect(list_slice(step)))
             if s == GROUP - 1:
                 src = picked[c][:].rearrange("p g n -> p (g n)").bitcast(I32)
@@ -101,19 +102,18 @@ def tile_list_rvq_silu_res_kernel(
                 queue.dma_start(dst[0:112, :], src[4:116, :])
 
         def gather_words(step):
-            if step == 0:
-                words = keep.tile([P, BLOCK], U32, name="words", tag="gate1", align_bytes=64)
-            else:
-                words = ring.tile([P, BLOCK], U32, name="words", bufs=2, align_bytes=64)
-            nc.vector.tensor_copy(words[:], tab_w[:].bitcast(U32).indirect(list_slice(step)))
+            width = 2 * BLOCK if step == 0 else BLOCK
+            tile = shared.tile([P, width], U32, name="words%d" % step, offset=2048 * (step % 2), align_bytes=64)
+            words = tile[:, 0:BLOCK]
+            nc.vector.tensor_copy(words, tab_w[:].bitcast(U32).indirect(list_slice(step)))
             return words
 
         def part(step, words):
-            if step in (2, 3):
-                parted = keep.tile([P, 2, 2 * BLOCK], U8, name="parted", tag="gate%d" % step, align_bytes=64)
-            else:
-                parted = ring.tile([P, 2, 2 * BLOCK], U8, name="parted", bufs=3, align_bytes=64)
-            nc.vector.tensor_copy(parted[:].bitcast(U16), words[:].bitcast(U16).rearrange("p (n d) -> p d n", d=2))
+            slot = step if step < 3 else (step - 1) % 3
+            rows = 4 if step == 2 else 2
+            tile = shared.tile([P, rows, 2 * BLOCK], U8, name="parted%d" % step, offset=3072 + 1024 * slot, align_bytes=64)
+            parted = tile[:, 0:2, :]
+            nc.vector.tensor_copy(parted.bitcast(U16), words.bitcast(U16).rearrange("p (n d) -> p d n", d=2))
             return parted
 
         acc = {}
@@ -142,7 +142,13 @@ def tile_list_rvq_silu_res_kernel(
         def activate(b, i):
             act = ring.tile([P, 4, P], F32, name="act", align_bytes=64)
             nc.scalar.activation(act[:], acc[b, i][:].rearrange("j (m t) -> j t m", t=4), ACT.Silu)
-            turned = psum.tile([P, 4, P], F32, name="turned", bufs=2)
+            return act
+
+        def turn(b, act):
+            if b == BLOCKS - 1:
+                turned = psum.tile([P, 4, P], F32, name="turned", tag="acc", bufs=4)
+            else:
+                turned = psum.tile([P, 4, P], F32, name="turned", bufs=2)
             for t in range(4):
                 nc.tensor.transpose(turned[:, t, :], act[:, t, :], ident[:])
             return turned
@@ -182,8 +188,8 @@ def tile_list_rvq_silu_res_kernel(
             gather_scales(step)
         load_weight(2)
         make_identity(nc, ident[:])
-        load_rest()
         hs = {}
+        last = BLOCKS - 1
         before = {3: (6,)}
         after = {1: (4,), 2: (5,), 3: (7,), 4: (8,), 5: (9, 10), 6: (11,)}
         words = gather_words(0)
@@ -197,19 +203,22 @@ def tile_list_rvq_silu_res_kernel(
             for s in after.get(step, ()):
                 gather_scales(s)
             if step == 3:
-                res_sb = keep.tile([P, 2, J], F32, name="res_sb", tag="gate3", align_bytes=64)
+                load_rest()
+                res_sb = keep.tile([P, 2, J], F32, name="res_sb", align_bytes=64)
                 nc.sync.dma_start(res_sb[:], res_v)
             if b > 0 and g == 0:
+                acts = [activate(b - 1, i) for i in range(TILES)]
+            if b > 0 and g == (0 if b == last else 1):
                 hs[b - 1] = ring.tile([P, BLOCK, 4], BF16, name="h", align_bytes=64)
-                turned = [activate(b - 1, i) for i in range(TILES)]
-                for i in range(TILES):
-                    smooth_scalar(turned[i], hs[b - 1][:, P * i : P * (i + 1), :])
-            if b == BLOCKS - 1 and g < LISTS - 1:
+                turned = [turn(b - 1, act) for act in acts]
+                smooth_scalar(turned[0], hs[b - 1][:, 0:P, :])
+                if b < last:
+                    smooth_scalar(turned[1], hs[b - 1][:, P:BLOCK, :])
+            if b == last and g < LISTS - 1:
                 finish(hs[g][:], g * BLOCK, BLOCK)
-        last = BLOCKS - 1
-        turned = [activate(last, i) for i in range(TILES)]
-        for b in range(last - 1, last):
-            finish(hs[b][:], b * BLOCK, BLOCK)
+        smooth_vector(turned[1], hs[last - 1][:, P:BLOCK, :])
+        turned = [turn(last, activate(last, i)) for i in range(TILES)]
+        finish(hs[last - 1][:], (last - 1) * BLOCK, BLOCK)
         h = ring.tile([P, BLOCK, 4], BF16, name="h", align_bytes=64)
         for i in range(TILES):
             smooth_vector(turned[i], h[:, P * i : P * (i + 1), :])

@@ -23,7 +23,11 @@ BLOCK = 256
 TILES = BLOCK // P
 BLOCKS = J // BLOCK
 STEPS = LISTS * BLOCKS
-GROUP = 4
+HALF = J // 2
+LAG = 3
+LINK = 64
+MAIN = 4 * BLOCK
+SECOND = 16
 
 
 def tile_list_rvq_silu_res_kernel(
@@ -35,10 +39,23 @@ def tile_list_rvq_silu_res_kernel(
     w_scales = (w0_scales, w1_scales, w2_scales)
     res_v = res.rearrange("(h p) j -> p h j", p=P)
     out_v = out.rearrange("(h p) j -> p h j", p=P)
+    last = BLOCKS - 1
+
+    scales_after = {(2, 0): 0, (0, 1): 3, (1, 1): 5, (2, 1): 6}
+    tenants = {step - LAG: HALF for step in scales_after.values() if step >= LAG}
+    tenants[4] = 2 * J * 4
+    place = {}
+    end = 0
+    for chain in range(LAG):
+        for step in range(chain, STEPS, LAG):
+            place[step] = end
+            end = end + LINK + MAIN + tenants.get(step, 0)
+        end = end + LINK
+    first_words = end
 
     with ExitStack() as ctx:
         keep = ctx.enter_context(tc.tile_pool(name="keep", bufs=1))
-        ring = ctx.enter_context(tc.tile_pool(name="ring", bufs=STEPS))
+        ring = ctx.enter_context(tc.tile_pool(name="ring", bufs=2 * BLOCKS))
         shared = ctx.enter_context(tc.tile_pool(name="shared", bufs=1))
         psum = ctx.enter_context(tc.psum_pool(name="psum", bufs=1))
 
@@ -46,93 +63,106 @@ def tile_list_rvq_silu_res_kernel(
         nc.sync.dma_start(offsets[:], offs)
 
         tab_s = keep.tile([P, T // 4], I32, name="tab_s", align_bytes=64)
-        nc.vector.memset(tab_s[:], 0)
-        sm_sb = keep.tile([P, 4], F32, name="sm_sb")
-        nc.sync.dma_start(sm_sb[:], sm.rearrange("(p t) -> p t", t=4))
-        ts = tab_scales.bitcast(I32)
-        for q in range(4):
-            nc.sync.dma_start(tab_s[32 * q : 32 * q + 8, :], ts[:, 4 * q : 4 * q + 4, :])
-        tab_w = keep.tile([P, T], I32, name="tab_w", align_bytes=64)
-        nc.sync.dma_start(tab_w[:], tab_words[0].rearrange("p n t -> p (n t)").bitcast(I32))
-
-        planes = keep.tile([P, (2 * LISTS * R + N) // 4], I32, name="planes", align_bytes=64)
-        nc.gpsimd.memset(planes[:, 256:512], 0)
-        nc.vector.memset(planes[:, 0:256], 0)
-        nc.vector.memset(planes[:, 512:], 0)
+        nc.gpsimd.memset(tab_s[:], 0)
+        width = 2 * R // 4
+        planes = keep.tile([P, LISTS * width + N // 4], I32, name="planes", align_bytes=64)
+        nc.vector.memset(planes[:], 0)
         moved_all = keep.tile([P, LISTS * J // 4], I32, name="moved_all", align_bytes=64)
         nc.vector.memset(moved_all[96:128, :], 0)
         ident = keep.tile([P, P], F32, name="ident", align_bytes=64)
+        make_identity(nc, ident[:])
 
-        w_sb = [keep.tile([P, 2, R], I32, name="w%d" % g, align_bytes=64) for g in range(LISTS)]
-        w_plane = [planes[:, g * 256 : (g + 1) * 256].rearrange("p (a n) -> p a n", a=2) for g in range(LISTS)]
+        w_sb = {g: keep.tile([P, 2, R], I32, name="w%d" % g, align_bytes=64) for g in range(2)}
+        w_plane = {g: planes[:, g * width : (g + 1) * width].rearrange("p (a n) -> p a n", a=2) for g in range(LISTS)}
+        wd_plane = planes[:, LISTS * width :]
+
+        def load_plane(g, queue):
+            src = w_scales[g].bitcast(I32)
+            for q in range(4):
+                queue.dma_start(w_plane[g][32 * q : 32 * q + 4, :, :],
+                                src[:, 4 * q : 4 * q + 4, :].rearrange("a r n -> r a n"))
 
         def load_weight(g):
             nc.sync.dma_start(w_sb[g][:], w_words[g].rearrange("a p n t -> p a (n t)").bitcast(I32))
-            src = w_scales[g].bitcast(I32)
-            for q in range(4):
-                (nc.gpsimd if g == 1 else nc.sync).dma_start(
-                    w_plane[g][32 * q : 32 * q + 4, :, :], src[:, 4 * q : 4 * q + 4, :].rearrange("a r n -> r a n"))
 
-        wd_plane = planes[:, LISTS * 256 : LISTS * 256 + N // 4]
+        sm_sb = keep.tile([P, 4], F32, name="sm_sb")
+        nc.sync.dma_start(sm_sb[:], sm.rearrange("(p t) -> p t", t=4))
         wd_sb = keep.tile([P, 2 * N // 4], I32, name="wd_sb", align_bytes=64)
+        nc.sync.dma_start(wd_sb[:], wd_words[0].bitcast(I32))
+        rows = tab_scales.bitcast(I32).rearrange("a (q r) n -> r q a n", r=4)
+        for r in range(4):
+            nc.sync.dma_start(tab_s[r:P:SECOND, :], rows[r])
+        tab_w = keep.tile([P, T], I32, name="tab_w", align_bytes=64)
+        nc.sync.dma_start(tab_w[:], tab_words[0].rearrange("p n t -> p (n t)").bitcast(I32))
+        load_plane(0, nc.sync)
+        load_weight(0)
+        load_plane(1, nc.sync)
+        load_weight(1)
+        load_plane(2, nc.gpsimd)
+        for q in range(4):
+            nc.gpsimd.dma_start(wd_plane[32 * q : 32 * q + 4, :], wd_scales.bitcast(I32)[0, 4 * q : 4 * q + 4, :])
 
-        def load_rest():
-            nc.sync.dma_start(wd_sb[:], wd_words[0].bitcast(I32))
-            for q in range(4):
-                nc.sync.dma_start(wd_plane[32 * q : 32 * q + 4, :], wd_scales.bitcast(I32)[0, 4 * q : 4 * q + 4, :])
+        late_sizes = (HALF, LINK)
+        late_at = [first_words + MAIN + sum(late_sizes[:n]) for n in range(len(late_sizes))]
+        spare = sum(late_sizes)
 
         picked = {}
-        span = GROUP * BLOCK // 4
-        moved = moved_all[:].bitcast(U8).rearrange("p (s n) -> p s n", s=STEPS)
+        moved = {}
 
-        def list_slice(step):
-            b, g = divmod(step, LISTS)
-            first = (g * J + b * BLOCK) // 16
-            return offsets[:, first : first + BLOCK // 16]
-
-        def gather_scales(step):
-            c, s = divmod(step, GROUP)
-            if s == 0:
-                picked[c] = shared.tile([P, GROUP, BLOCK], U8, name="picked%d" % c, offset=(7168, 1024, 6144)[c], align_bytes=64)
-            nc.vector.tensor_copy(picked[c][:, s, :], tab_s[:].bitcast(U8).indirect(list_slice(step)))
-            if s == GROUP - 1:
-                src = picked[c][:].rearrange("p g n -> p (g n)").bitcast(I32)
-                dst = moved_all[:, c * span : (c + 1) * span]
-                queue = nc.scalar if c == 0 else nc.sync
-                queue.dma_start(dst[0:112, :], src[4:116, :])
+        def gather_scales(g, half):
+            name = "picked%d_%d" % (g, half)
+            after = scales_after.get((g, half))
+            if after is None:
+                tile = keep.tile([P, HALF], U8, name=name, align_bytes=64)
+            elif after < LAG:
+                tile = shared.tile([P, HALF], U8, name=name, offset=first_words + MAIN, align_bytes=64)
+            else:
+                tile = shared.tile([P, HALF], U8, name=name, offset=place[after - LAG] + LINK + MAIN, align_bytes=64)
+            first = (g * J + half * HALF) // 16
+            nc.vector.tensor_copy(tile[:], tab_s[:].bitcast(U8).indirect(offsets[:, first : first + HALF // 16]))
+            at = (half * LISTS + g) * HALF // 4
+            dst = moved_all[:, at : at + HALF // 4]
+            queue = nc.scalar if half == 0 else nc.sync
+            queue.dma_start(dst[0 : P - SECOND, :], tile[:].bitcast(I32)[SECOND:P, :])
+            picked[g, half] = tile[:]
+            moved[g, half] = dst.bitcast(U8)
 
         def gather_words(step):
-            width = 2 * BLOCK if step == 0 else BLOCK
-            tile = shared.tile([P, width], U32, name="words%d" % step, offset=2048 * (step % 2), align_bytes=64)
+            b, g = divmod(step, LISTS)
+            if step == 0:
+                tile = shared.tile([P, BLOCK + spare // 4], U32, name="words0", offset=first_words, align_bytes=64)
+            elif step <= LAG:
+                tile = shared.tile([P, BLOCK], U32, name="words%d" % step,
+                                   offset=first_words + (MAIN + spare + 8 * R) * (step % 2), align_bytes=64)
+            else:
+                tile = shared.tile([P, BLOCK], U32, name="words%d" % step,
+                                   offset=place[step - 1 - LAG] + LINK, align_bytes=64)
+            first = (g * J + b * BLOCK) // 16
             words = tile[:, 0:BLOCK]
-            nc.vector.tensor_copy(words, tab_w[:].bitcast(U32).indirect(list_slice(step)))
+            nc.vector.tensor_copy(words, tab_w[:].bitcast(U32).indirect(offsets[:, first : first + BLOCK // 16]))
             return words
 
         def part(step, words):
-            slot = step if step < 3 else (step - 1) % 3
-            rows = 4 if step == 2 else 2
-            tile = shared.tile([P, rows, 2 * BLOCK], U8, name="parted%d" % step, offset=3072 + 1024 * slot, align_bytes=64)
-            parted = tile[:, 0:2, :]
+            size = LINK + MAIN + tenants.get(step, 0) + LINK
+            tile = shared.tile([P, size], U8, name="parted%d" % step, offset=place[step], align_bytes=64)
+            parted = tile[:, LINK : LINK + MAIN].rearrange("p (a n) -> p a n", a=2)
             nc.vector.tensor_copy(parted.bitcast(U16), words.bitcast(U16).rearrange("p (n d) -> p d n", d=2))
             return parted
 
         acc = {}
+        parts = {}
 
-        def project(step, parted):
+        def project(step, i):
             b, g = divmod(step, LISTS)
+            half, at = divmod(b * BLOCK + i * P, HALF)
             if g == 0:
-                for i in range(TILES):
-                    acc[b, i] = psum.tile([P, R], F32, name="acc", bufs=4)
-            if step == STEPS - 1:
-                order = [(a, i) for i in range(TILES) for a in range(2)]
-            else:
-                order = [(a, i) for a in range(2) for i in range(TILES)]
-            for a, i in order:
-                plane = (picked[step // GROUP][:, step % GROUP, :], moved[:, step, :])[a]
+                acc[b, i] = psum.tile([P, R], F32, name="acc", bufs=4)
+            for a in range(2):
+                plane = (picked, moved)[a][g, half]
                 nc.tensor.matmul_mx(
                     out=acc[b, i][:],
-                    lhsT=parted[:, a, 2 * P * i : 2 * P * (i + 1)].bitcast(FP4X4),
-                    lhsT_scale=plane[:, P * i : P * (i + 1)],
+                    lhsT=parts[step][:, a, 2 * P * i : 2 * P * (i + 1)].bitcast(FP4X4),
+                    lhsT_scale=plane[:, at : at + P],
                     rhs=w_sb[g][:, a, :].bitcast(FP8X4),
                     rhs_scale=w_plane[g][:, a, :].bitcast(U8),
                     start=(g == 0 and a == 0),
@@ -145,7 +175,7 @@ def tile_list_rvq_silu_res_kernel(
             return act
 
         def turn(b, act):
-            if b == BLOCKS - 1:
+            if b == last:
                 turned = psum.tile([P, 4, P], F32, name="turned", tag="acc", bufs=4)
             else:
                 turned = psum.tile([P, 4, P], F32, name="turned", bufs=2)
@@ -154,20 +184,24 @@ def tile_list_rvq_silu_res_kernel(
             return turned
 
         def smooth_scalar(turned, h_cols):
-            rows = ring.tile([P, 4, P], BF16, name="rows", align_bytes=64)
+            flat = ring.tile([P, 4, P], BF16, name="flat", align_bytes=64)
             for t in range(4):
-                nc.scalar.activation(rows[:, t, :], turned[:, t, :], ACT.Copy, scale=sm_sb[:, t : t + 1])
-            nc.scalar.copy(h_cols, rows[:].rearrange("p t j -> p j t"))
+                nc.scalar.activation(flat[:, t, :], turned[:, t, :], ACT.Copy, scale=sm_sb[:, t : t + 1])
+            nc.scalar.copy(h_cols, flat[:].rearrange("p t j -> p j t"))
 
         def smooth_vector(turned, h_cols):
             nc.vector.tensor_tensor(h_cols, turned[:].rearrange("p t j -> p j t"),
                                     sm_sb[:].unsqueeze(1).to_broadcast([P, P, 4]), ALU.mult)
 
-        def finish(h, first, width):
-            codes = ring.tile([P, width], U32, name="codes", align_bytes=64)
-            scales = ring.tile([P, width], U8, name="scales", align_bytes=64)
+        def quantise(h, cols):
+            codes = ring.tile([P, cols], U32, name="codes", align_bytes=64)
+            scales = ring.tile([P, cols], U8, name="scales", align_bytes=64)
             nc.vector.quantize_mx(out=codes[:].bitcast(FP8X4), scales=scales[:], in_=h.rearrange("p j t -> p (j t)"))
-            y = psum.tile([P, 2, width], F32, name="y", bufs=2)
+            return codes, scales
+
+        def finish(operand, first, cols):
+            codes, scales = operand
+            y = psum.tile([P, 2, cols], F32, name="y", bufs=2)
             for half in range(2):
                 nc.tensor.matmul_mx(
                     out=y[:, half, :],
@@ -178,49 +212,59 @@ def tile_list_rvq_silu_res_kernel(
                     start=True,
                     stop=True,
                 )
-            result = ring.tile([P, 2, width], F32, name="result")
-            nc.vector.tensor_tensor(result[:], y[:], res_sb[:, :, first : first + width], ALU.add)
-            nc.sync.dma_start(out_v[:, :, first : first + width], result[:])
+            result = ring.tile([P, 2, cols], F32, name="result")
+            nc.vector.tensor_tensor(result[:], y[:], res_sb[:, :, first : first + cols], ALU.add)
+            nc.sync.dma_start(out_v[:, :, first : first + cols], result[:])
 
-        load_weight(0)
-        load_weight(1)
-        for step in range(GROUP):
-            gather_scales(step)
-        load_weight(2)
-        make_identity(nc, ident[:])
+        def new_h():
+            return ring.tile([P, BLOCK, 4], BF16, name="h", align_bytes=64)
+
+        gather_scales(0, 0)
+        gather_scales(1, 0)
         hs = {}
-        last = BLOCKS - 1
-        before = {3: (6,)}
-        after = {1: (4,), 2: (5,), 3: (7,), 4: (8,), 5: (9, 10), 6: (11,)}
+        operand = {}
         words = gather_words(0)
         for step in range(STEPS):
             b, g = divmod(step, LISTS)
             ahead = gather_words(step + 1) if step + 1 < STEPS else None
-            for s in before.get(step, ()):
-                gather_scales(s)
-            project(step, part(step, words))
+            parts[step] = part(step, words)
             words = ahead
-            for s in after.get(step, ()):
-                gather_scales(s)
-            if step == 3:
-                load_rest()
-                res_sb = keep.tile([P, 2, J], F32, name="res_sb", align_bytes=64)
+            if step == 0:
+                w_sb[2] = shared.tile([P, 2, R], I32, name="w2", offset=late_at[1], align_bytes=64)
+                load_weight(2)
+            for key in scales_after:
+                if scales_after[key] == step:
+                    gather_scales(*key)
+            if step == 4 + LAG:
+                res_sb = shared.tile([P, 2, J], F32, name="res_sb", offset=place[4] + LINK + MAIN, align_bytes=64)
                 nc.sync.dma_start(res_sb[:], res_v)
-            if b > 0 and g == 0:
-                acts = [activate(b - 1, i) for i in range(TILES)]
-            if b > 0 and g == (0 if b == last else 1):
-                hs[b - 1] = ring.tile([P, BLOCK, 4], BF16, name="h", align_bytes=64)
-                turned = [turn(b - 1, act) for act in acts]
-                smooth_scalar(turned[0], hs[b - 1][:, 0:P, :])
-                if b < last:
-                    smooth_scalar(turned[1], hs[b - 1][:, P:BLOCK, :])
-            if b == last and g < LISTS - 1:
-                finish(hs[g][:], g * BLOCK, BLOCK)
-        smooth_vector(turned[1], hs[last - 1][:, P:BLOCK, :])
-        turned = [turn(last, activate(last, i)) for i in range(TILES)]
-        finish(hs[last - 1][:], (last - 1) * BLOCK, BLOCK)
-        h = ring.tile([P, BLOCK, 4], BF16, name="h", align_bytes=64)
-        for i in range(TILES):
-            smooth_vector(turned[i], h[:, P * i : P * (i + 1), :])
-        for i in range(TILES):
-            finish(h[:, P * i : P * (i + 1), :], last * BLOCK + P * i, P)
+            if b < last:
+                for i in range(TILES):
+                    project(step, i)
+                if g == LISTS - 1:
+                    acts = [activate(b, i) for i in range(TILES)]
+                if b > 0 and g == 0:
+                    hs[b - 1] = new_h()
+                    for i in range(TILES):
+                        smooth_scalar(turn(b - 1, acts[i]), hs[b - 1][:, P * i : P * (i + 1), :])
+                if step == 3 * last - 1:
+                    finish(quantise(hs[0][:], BLOCK), 0, BLOCK)
+        operand[1] = quantise(hs[1][:], BLOCK)
+        for g in range(LISTS):
+            project(3 * last + g, 0)
+        act_a = activate(last, 0)
+        hs[2] = new_h()
+        hs[3] = new_h()
+        turned = [turn(last - 1, act) for act in acts]
+        smooth_scalar(turned[0], hs[2][:, 0:P, :])
+        smooth_vector(turned[1], hs[2][:, P:BLOCK, :])
+        smooth_vector(turn(last, act_a), hs[3][:, 0:P, :])
+        project(3 * last, 1)
+        finish(operand[1], BLOCK, BLOCK)
+        project(3 * last + 1, 1)
+        project(3 * last + 2, 1)
+        act_b = activate(last, 1)
+        finish(quantise(hs[2][:], BLOCK), 2 * BLOCK, BLOCK)
+        finish(quantise(hs[3][:, 0:P, :], P), last * BLOCK, P)
+        smooth_vector(turn(last, act_b), hs[3][:, P:BLOCK, :])
+        finish(quantise(hs[3][:, P:BLOCK, :], P), last * BLOCK + P, P)

@@ -1,7 +1,6 @@
 from contextlib import ExitStack
 
 import concourse.mybir as mybir
-from concourse.masks import make_identity
 
 K, R, N, T, J = 1024, 512, 256, 2048, 1024
 FLOPS = 2 * (3 * K * R * J + R * N * J)
@@ -41,9 +40,11 @@ def tile_list_rvq_silu_res_kernel(
     out_v = out.rearrange("(h p) j -> p h j", p=P)
     last = BLOCKS - 1
 
-    scales_after = {(2, 0): 0, (0, 1): 3, (1, 1): 5, (2, 1): 6}
-    tenants = {step - LAG: HALF for step in scales_after.values() if step >= LAG}
+    scales_after = {3: 0, 5: 1, 6: 2}
+    tenants = {step - LAG: HALF for step in scales_after}
     tenants[4] = 2 * J * 4
+    tenants[0] = 0
+    tenants[1] = 3 * N + LINK
     place = {}
     end = 0
     for chain in range(LAG):
@@ -52,6 +53,7 @@ def tile_list_rvq_silu_res_kernel(
             end = end + LINK + MAIN + tenants.get(step, 0)
         end = end + LINK
     first_words = end
+    raw_at = {2: first_words + MAIN, 0: first_words + 2 * MAIN + 8 * R, 1: first_words + 2 * MAIN + 16 * R}
 
     with ExitStack() as ctx:
         keep = ctx.enter_context(tc.tile_pool(name="keep", bufs=1))
@@ -64,76 +66,69 @@ def tile_list_rvq_silu_res_kernel(
 
         tab_s = keep.tile([P, T // 4], I32, name="tab_s", align_bytes=64)
         nc.gpsimd.memset(tab_s[:], 0)
-        width = 2 * R // 4
-        planes = keep.tile([P, LISTS * width + N // 4], I32, name="planes", align_bytes=64)
+        staged = keep.tile([P, LISTS, R // 4], I32, name="staged", align_bytes=64)
+        for g in range(LISTS):
+            nc.sync.dma_start(staged[0:32, g, :], w_scales[g].bitcast(I32).rearrange("a q n -> (a q) n"))
+        nc.vector.memset(staged[32:64], 0)
+        nc.vector.memset(staged[64:128], 0)
+        planes = keep.tile([P, 2, LISTS * R // 4], I32, name="planes", align_bytes=64)
         nc.vector.memset(planes[:], 0)
         moved_all = keep.tile([P, LISTS * J // 4], I32, name="moved_all", align_bytes=64)
-        nc.vector.memset(moved_all[96:128, :], 0)
-        ident = keep.tile([P, P], F32, name="ident", align_bytes=64)
-        make_identity(nc, ident[:])
+        nc.gpsimd.memset(moved_all[96:128, :], 0)
 
-        w_sb = {g: keep.tile([P, 2, R], I32, name="w%d" % g, align_bytes=64) for g in range(2)}
-        w_plane = {g: planes[:, g * width : (g + 1) * width].rearrange("p (a n) -> p a n", a=2) for g in range(LISTS)}
-        wd_plane = planes[:, LISTS * width :]
-
-        def load_plane(g, queue):
-            src = w_scales[g].bitcast(I32)
-            for q in range(4):
-                queue.dma_start(w_plane[g][32 * q : 32 * q + 4, :, :],
-                                src[:, 4 * q : 4 * q + 4, :].rearrange("a r n -> r a n"))
+        w_sb = {g: shared.tile([P, 2, R], I32, name="w%d" % g, offset=raw_at[g], align_bytes=64) for g in range(2)}
 
         def load_weight(g):
             nc.sync.dma_start(w_sb[g][:], w_words[g].rearrange("a p n t -> p a (n t)").bitcast(I32))
 
-        sm_sb = keep.tile([P, 4], F32, name="sm_sb")
-        nc.sync.dma_start(sm_sb[:], sm.rearrange("(p t) -> p t", t=4))
-        wd_sb = keep.tile([P, 2 * N // 4], I32, name="wd_sb", align_bytes=64)
-        nc.sync.dma_start(wd_sb[:], wd_words[0].bitcast(I32))
         rows = tab_scales.bitcast(I32).rearrange("a (q r) n -> r q a n", r=4)
         for r in range(4):
             nc.sync.dma_start(tab_s[r:P:SECOND, :], rows[r])
         tab_w = keep.tile([P, T], I32, name="tab_w", align_bytes=64)
         nc.sync.dma_start(tab_w[:], tab_words[0].rearrange("p n t -> p (n t)").bitcast(I32))
-        load_plane(0, nc.sync)
         load_weight(0)
-        load_plane(1, nc.sync)
         load_weight(1)
-        load_plane(2, nc.gpsimd)
-        for q in range(4):
-            nc.gpsimd.dma_start(wd_plane[32 * q : 32 * q + 4, :], wd_scales.bitcast(I32)[0, 4 * q : 4 * q + 4, :])
 
-        late_sizes = (HALF, LINK)
-        late_at = [first_words + MAIN + sum(late_sizes[:n]) for n in range(len(late_sizes))]
-        spare = sum(late_sizes)
+        dealt = {}
+
+        def deal(g):
+            dealt[g] = keep.tile([P, 2, R], U32, name="dealt%d" % g, align_bytes=64)
+            nc.vector.tensor_copy(dealt[g][:].rearrange("p a (t c i) -> p a c t i", t=4, i=4),
+                                  w_sb[g][:].bitcast(U32).rearrange("p a (c i t) -> p a c t i", t=4, i=4))
+
+        def deal_scales():
+            tile = keep.tile([P, LISTS * R], U8, name="dealt_scales", align_bytes=64)
+            nc.vector.tensor_copy(tile[:].rearrange("p (g t c i) -> p c g t i", g=LISTS, t=4, i=16),
+                                  staged[:].bitcast(U8).rearrange("p g (c i t) -> p c g t i", t=4, i=16))
+            for a in range(2):
+                for q in range(4):
+                    row = 16 * a + 4 * q
+                    nc.scalar.dma_start(planes[32 * q : 32 * q + 4, a, :], tile[:].bitcast(I32)[row : row + 4, :])
 
         picked = {}
         moved = {}
 
-        def gather_scales(g, half):
-            name = "picked%d_%d" % (g, half)
-            after = scales_after.get((g, half))
-            if after is None:
-                tile = keep.tile([P, HALF], U8, name=name, align_bytes=64)
-            elif after < LAG:
-                tile = shared.tile([P, HALF], U8, name=name, offset=first_words + MAIN, align_bytes=64)
-            else:
-                tile = shared.tile([P, HALF], U8, name=name, offset=place[after - LAG] + LINK + MAIN, align_bytes=64)
-            first = (g * J + half * HALF) // 16
-            nc.vector.tensor_copy(tile[:], tab_s[:].bitcast(U8).indirect(offsets[:, first : first + HALF // 16]))
-            at = (half * LISTS + g) * HALF // 4
-            dst = moved_all[:, at : at + HALF // 4]
-            queue = nc.scalar if half == 0 else nc.sync
+        def gather_scales(lists, half, tile, queue):
+            at = (half * LISTS + lists[0]) * HALF // 4
+            dst = moved_all[:, at : at + len(lists) * HALF // 4]
+            for n, g in enumerate(lists):
+                first = (g * J + half * HALF) // 16
+                picked[g, half] = tile[:, n * HALF : (n + 1) * HALF]
+                moved[g, half] = dst.bitcast(U8)[:, n * HALF : (n + 1) * HALF]
+                nc.vector.tensor_copy(picked[g, half], tab_s[:].bitcast(U8).indirect(offsets[:, first : first + HALF // 16]))
             queue.dma_start(dst[0 : P - SECOND, :], tile[:].bitcast(I32)[SECOND:P, :])
-            picked[g, half] = tile[:]
-            moved[g, half] = dst.bitcast(U8)
 
         def gather_words(step):
             b, g = divmod(step, LISTS)
             if step == 0:
-                tile = shared.tile([P, BLOCK + spare // 4], U32, name="words0", offset=first_words, align_bytes=64)
+                tile = shared.tile([P, BLOCK + LINK // 4], U32, name="words0", offset=first_words, align_bytes=64)
+            elif step == 1:
+                tile = shared.tile([P, BLOCK], U32, name="words1", offset=first_words + MAIN + 8 * R, align_bytes=64)
             elif step <= LAG:
+                tile = shared.tile([P, BLOCK], U32, name="words%d" % step, offset=raw_at[step - 2], align_bytes=64)
+            elif step <= LAG + 2:
                 tile = shared.tile([P, BLOCK], U32, name="words%d" % step,
-                                   offset=first_words + (MAIN + spare + 8 * R) * (step % 2), align_bytes=64)
+                                   offset=raw_at[2] + MAIN * (step - LAG), align_bytes=64)
             else:
                 tile = shared.tile([P, BLOCK], U32, name="words%d" % step,
                                    offset=place[step - 1 - LAG] + LINK, align_bytes=64)
@@ -152,45 +147,38 @@ def tile_list_rvq_silu_res_kernel(
         acc = {}
         parts = {}
 
-        def project(step, i):
+        def project(step):
             b, g = divmod(step, LISTS)
-            half, at = divmod(b * BLOCK + i * P, HALF)
-            if g == 0:
-                acc[b, i] = psum.tile([P, R], F32, name="acc", bufs=4)
-            for a in range(2):
-                plane = (picked, moved)[a][g, half]
-                nc.tensor.matmul_mx(
-                    out=acc[b, i][:],
-                    lhsT=parts[step][:, a, 2 * P * i : 2 * P * (i + 1)].bitcast(FP4X4),
-                    lhsT_scale=plane[:, at : at + P],
-                    rhs=w_sb[g][:, a, :].bitcast(FP8X4),
-                    rhs_scale=w_plane[g][:, a, :].bitcast(U8),
-                    start=(g == 0 and a == 0),
-                    stop=(g == LISTS - 1 and a == 1),
-                )
+            half, at = divmod(b * BLOCK, HALF)
+            for t in range(4):
+                if g == 0:
+                    acc[b, t] = psum.tile([P, BLOCK], F32, name="acc", tag="bank", bufs=8)
+                for a in range(2):
+                    for i in range(TILES):
+                        nc.tensor.matmul_mx(
+                            out=acc[b, t][:, P * i : P * (i + 1)],
+                            lhsT=dealt[g][:, a, P * t : P * (t + 1)].bitcast(FP8X4),
+                            lhsT_scale=planes[:, a, :].bitcast(U8)[:, g * R + P * t : g * R + P * (t + 1)],
+                            rhs=parts[step][:, a, 2 * P * i : 2 * P * (i + 1)].bitcast(FP4X4),
+                            rhs_scale=(picked, moved)[a][g, half][:, at + P * i : at + P * (i + 1)],
+                            start=(g == 0 and a == 0 and i == 0),
+                            stop=(g == LISTS - 1 and a == 1 and i == TILES - 1),
+                        )
 
-        def activate(b, i):
-            act = ring.tile([P, 4, P], F32, name="act", align_bytes=64)
-            nc.scalar.activation(act[:], acc[b, i][:].rearrange("j (m t) -> j t m", t=4), ACT.Silu)
+        def activate(b):
+            act = ring.tile([P, 4, BLOCK], F32, name="act", align_bytes=64)
+            for t in range(4):
+                nc.scalar.activation(act[:, t, :], acc[b, t][:], ACT.Silu)
             return act
 
-        def turn(b, act):
-            if b == last:
-                turned = psum.tile([P, 4, P], F32, name="turned", tag="acc", bufs=4)
-            else:
-                turned = psum.tile([P, 4, P], F32, name="turned", bufs=2)
+        def smooth_scalar(act, h_cols):
+            flat = ring.tile(list(act.shape), BF16, name="flat", align_bytes=64)
             for t in range(4):
-                nc.tensor.transpose(turned[:, t, :], act[:, t, :], ident[:])
-            return turned
+                nc.scalar.activation(flat[:, t, :], act[:, t, :], ACT.Copy, scale=sm_sb[:, t : t + 1])
+            nc.scalar.copy(h_cols.rearrange("p (c i) t -> p c t i", i=4), flat[:].rearrange("p t (c i) -> p c t i", i=4))
 
-        def smooth_scalar(turned, h_cols):
-            flat = ring.tile([P, 4, P], BF16, name="flat", align_bytes=64)
-            for t in range(4):
-                nc.scalar.activation(flat[:, t, :], turned[:, t, :], ACT.Copy, scale=sm_sb[:, t : t + 1])
-            nc.scalar.copy(h_cols, flat[:].rearrange("p t j -> p j t"))
-
-        def smooth_vector(turned, h_cols):
-            nc.vector.tensor_tensor(h_cols, turned[:].rearrange("p t j -> p j t"),
+        def smooth_vector(act, h_cols):
+            nc.vector.tensor_tensor(h_cols, act.rearrange("p t j -> p j t"),
                                     sm_sb[:].unsqueeze(1).to_broadcast([P, P, 4]), ALU.mult)
 
         def quantise(h, cols):
@@ -201,7 +189,7 @@ def tile_list_rvq_silu_res_kernel(
 
         def finish(operand, first, cols):
             codes, scales = operand
-            y = psum.tile([P, 2, cols], F32, name="y", bufs=2)
+            y = psum.tile([P, 2, cols], F32, name="y", tag="bank", bufs=8)
             for half in range(2):
                 nc.tensor.matmul_mx(
                     out=y[:, half, :],
@@ -219,8 +207,8 @@ def tile_list_rvq_silu_res_kernel(
         def new_h():
             return ring.tile([P, BLOCK, 4], BF16, name="h", align_bytes=64)
 
-        gather_scales(0, 0)
-        gather_scales(1, 0)
+        gather_scales((0, 1, 2), 0, keep.tile([P, LISTS * HALF], U8, name="picked_first", align_bytes=64), nc.scalar)
+        deal_scales()
         hs = {}
         operand = {}
         words = gather_words(0)
@@ -230,41 +218,47 @@ def tile_list_rvq_silu_res_kernel(
             parts[step] = part(step, words)
             words = ahead
             if step == 0:
-                w_sb[2] = shared.tile([P, 2, R], I32, name="w2", offset=late_at[1], align_bytes=64)
+                w_sb[2] = shared.tile([P, 2, R], I32, name="w2", offset=raw_at[2], align_bytes=64)
                 load_weight(2)
-            for key in scales_after:
-                if scales_after[key] == step:
-                    gather_scales(*key)
+            if step == 1:
+                deal(0)
+            if step in scales_after:
+                tile = shared.tile([P, HALF], U8, name="picked%d" % step,
+                                   offset=raw_at[2] + 3 * MAIN if step == LAG else place[step - LAG] + LINK + MAIN,
+                                   align_bytes=64)
+                gather_scales((scales_after[step],), 1, tile, nc.sync)
+            if step == 1:
+                wd_plane = shared.tile([P, N // 4], I32, name="wd_plane", offset=place[1] + LINK + MAIN, align_bytes=64)[:]
+                nc.gpsimd.memset(wd_plane, 0)
+                sm_sb = shared.tile([P, 4], F32, name="sm_sb", offset=place[1] + LINK + MAIN + 3 * N, align_bytes=64)
+                nc.sync.dma_start(sm_sb[:], sm.rearrange("(p t) -> p t", t=4))
+                wd_sb = shared.tile([P, 2 * N // 4], I32, name="wd_sb", offset=place[1] + LINK + MAIN + N, align_bytes=64)
+                nc.sync.dma_start(wd_sb[:], wd_words[0].bitcast(I32))
+                for q in range(4):
+                    nc.sync.dma_start(wd_plane[32 * q : 32 * q + 4, :], wd_scales.bitcast(I32)[0, 4 * q : 4 * q + 4, :])
             if step == 4 + LAG:
                 res_sb = shared.tile([P, 2, J], F32, name="res_sb", offset=place[4] + LINK + MAIN, align_bytes=64)
                 nc.sync.dma_start(res_sb[:], res_v)
-            if b < last:
-                for i in range(TILES):
-                    project(step, i)
-                if g == LISTS - 1:
-                    acts = [activate(b, i) for i in range(TILES)]
-                if b > 0 and g == 0:
-                    hs[b - 1] = new_h()
-                    for i in range(TILES):
-                        smooth_scalar(turn(b - 1, acts[i]), hs[b - 1][:, P * i : P * (i + 1), :])
-                if step == 3 * last - 1:
-                    finish(quantise(hs[0][:], BLOCK), 0, BLOCK)
-        operand[1] = quantise(hs[1][:], BLOCK)
-        for g in range(LISTS):
-            project(3 * last + g, 0)
-        act_a = activate(last, 0)
-        hs[2] = new_h()
-        hs[3] = new_h()
-        turned = [turn(last - 1, act) for act in acts]
-        smooth_scalar(turned[0], hs[2][:, 0:P, :])
-        smooth_vector(turned[1], hs[2][:, P:BLOCK, :])
-        smooth_vector(turn(last, act_a), hs[3][:, 0:P, :])
-        project(3 * last, 1)
+            if step == 1:
+                project(0)
+                deal(1)
+            if step == 2:
+                deal(2)
+            if step > 0:
+                project(step)
+            if g == LISTS - 1:
+                act = activate(b)
+                hs[b] = new_h()
+                if b < last:
+                    smooth_scalar(act[:], hs[b][:])
+            if step == 3 * last - 1:
+                finish(quantise(hs[0][:], BLOCK), 0, BLOCK)
+            if step == STEPS - 2:
+                operand[1] = quantise(hs[1][:], BLOCK)
         finish(operand[1], BLOCK, BLOCK)
-        project(3 * last + 1, 1)
-        project(3 * last + 2, 1)
-        act_b = activate(last, 1)
         finish(quantise(hs[2][:], BLOCK), 2 * BLOCK, BLOCK)
-        finish(quantise(hs[3][:, 0:P, :], P), last * BLOCK, P)
-        smooth_vector(turn(last, act_b), hs[3][:, P:BLOCK, :])
-        finish(quantise(hs[3][:, P:BLOCK, :], P), last * BLOCK + P, P)
+        for i in range(TILES):
+            smooth_vector(act[:, :, P * i : P * (i + 1)], hs[last][:, P * i : P * (i + 1), :])
+        tail = [quantise(hs[last][:, P * i : P * (i + 1), :], P) for i in range(TILES)]
+        for i in range(TILES):
+            finish(tail[i], last * BLOCK + P * i, P)

@@ -53,7 +53,8 @@ def tile_list_rvq_silu_res_kernel(
             end = end + LINK + MAIN + tenants.get(step, 0)
         end = end + LINK
     first_words = end
-    raw_at = {2: first_words + MAIN, 0: first_words + 2 * MAIN + 8 * R, 1: first_words + 2 * MAIN + 16 * R}
+    raw_at = {2: first_words + MAIN, 0: first_words + MAIN + 8 * R, 1: first_words + MAIN + 16 * R}
+    place[0] = raw_at[0] + 8 * R - MAIN - 2 * LINK
 
     with ExitStack() as ctx:
         keep = ctx.enter_context(tc.tile_pool(name="keep", bufs=1))
@@ -68,7 +69,7 @@ def tile_list_rvq_silu_res_kernel(
         nc.gpsimd.memset(tab_s[:], 0)
         staged = keep.tile([P, LISTS, R // 4], I32, name="staged", align_bytes=64)
         for g in range(LISTS):
-            nc.sync.dma_start(staged[0:32, g, :], w_scales[g].bitcast(I32).rearrange("a q n -> (a q) n"))
+            nc.sync.dma_start(staged[0:32, g, :], w_scales[g].bitcast(I32).rearrange("a q n -> q a n"))
         nc.vector.memset(staged[32:64], 0)
         nc.vector.memset(staged[64:128], 0)
         planes = keep.tile([P, 2, LISTS * R // 4], I32, name="planes", align_bytes=64)
@@ -76,7 +77,7 @@ def tile_list_rvq_silu_res_kernel(
         moved_all = keep.tile([P, LISTS * J // 4], I32, name="moved_all", align_bytes=64)
         nc.gpsimd.memset(moved_all[96:128, :], 0)
 
-        w_sb = {g: shared.tile([P, 2, R], I32, name="w%d" % g, offset=raw_at[g], align_bytes=64) for g in range(2)}
+        w_sb = {g: shared.tile([P, 2, R], I32, name="w%d" % g, offset=raw_at[g], align_bytes=64) for g in range(LISTS)}
 
         def load_weight(g):
             nc.sync.dma_start(w_sb[g][:], w_words[g].rearrange("a p n t -> p a (n t)").bitcast(I32))
@@ -88,6 +89,7 @@ def tile_list_rvq_silu_res_kernel(
         nc.sync.dma_start(tab_w[:], tab_words[0].rearrange("p n t -> p (n t)").bitcast(I32))
         load_weight(0)
         load_weight(1)
+        load_weight(2)
 
         dealt = {}
 
@@ -100,10 +102,8 @@ def tile_list_rvq_silu_res_kernel(
             tile = keep.tile([P, LISTS * R], U8, name="dealt_scales", align_bytes=64)
             nc.vector.tensor_copy(tile[:].rearrange("p (g t c i) -> p c g t i", g=LISTS, t=4, i=16),
                                   staged[:].bitcast(U8).rearrange("p g (c i t) -> p c g t i", t=4, i=16))
-            for a in range(2):
-                for q in range(4):
-                    row = 16 * a + 4 * q
-                    nc.scalar.dma_start(planes[32 * q : 32 * q + 4, a, :], tile[:].bitcast(I32)[row : row + 4, :])
+            for q in range(4):
+                nc.scalar.dma_start(planes[32 * q : 32 * q + 4], tile[:].bitcast(I32)[8 * q : 8 * q + 8, :])
 
         picked = {}
         moved = {}
@@ -121,11 +121,11 @@ def tile_list_rvq_silu_res_kernel(
         def gather_words(step):
             b, g = divmod(step, LISTS)
             if step == 0:
-                tile = shared.tile([P, BLOCK + LINK // 4], U32, name="words0", offset=first_words, align_bytes=64)
-            elif step == 1:
-                tile = shared.tile([P, BLOCK], U32, name="words1", offset=first_words + MAIN + 8 * R, align_bytes=64)
-            elif step <= LAG:
-                tile = shared.tile([P, BLOCK], U32, name="words%d" % step, offset=raw_at[step - 2], align_bytes=64)
+                tile = shared.tile([P, BLOCK], U32, name="words0", offset=first_words, align_bytes=64)
+            elif step < LAG:
+                tile = shared.tile([P, BLOCK], U32, name="words%d" % step, offset=raw_at[0] + MAIN * (step - 1), align_bytes=64)
+            elif step == LAG:
+                tile = shared.tile([P, BLOCK], U32, name="words%d" % step, offset=raw_at[1], align_bytes=64)
             elif step <= LAG + 2:
                 tile = shared.tile([P, BLOCK], U32, name="words%d" % step,
                                    offset=raw_at[2] + MAIN * (step - LAG), align_bytes=64)
@@ -207,21 +207,19 @@ def tile_list_rvq_silu_res_kernel(
         def new_h():
             return ring.tile([P, BLOCK, 4], BF16, name="h", align_bytes=64)
 
-        gather_scales((0, 1, 2), 0, keep.tile([P, LISTS * HALF], U8, name="picked_first", align_bytes=64), nc.scalar)
         deal_scales()
+        gather_scales((0, 1, 2), 0, keep.tile([P, LISTS * HALF], U8, name="picked_first", align_bytes=64), nc.scalar)
         hs = {}
         operand = {}
         words = gather_words(0)
+        deal(0)
+        parts[0] = part(0, words)
         for step in range(STEPS):
             b, g = divmod(step, LISTS)
             ahead = gather_words(step + 1) if step + 1 < STEPS else None
-            parts[step] = part(step, words)
+            if step > 0:
+                parts[step] = part(step, words)
             words = ahead
-            if step == 0:
-                w_sb[2] = shared.tile([P, 2, R], I32, name="w2", offset=raw_at[2], align_bytes=64)
-                load_weight(2)
-            if step == 1:
-                deal(0)
             if step in scales_after:
                 tile = shared.tile([P, HALF], U8, name="picked%d" % step,
                                    offset=raw_at[2] + 3 * MAIN if step == LAG else place[step - LAG] + LINK + MAIN,
@@ -239,26 +237,26 @@ def tile_list_rvq_silu_res_kernel(
             if step == 4 + LAG:
                 res_sb = shared.tile([P, 2, J], F32, name="res_sb", offset=place[4] + LINK + MAIN, align_bytes=64)
                 nc.sync.dma_start(res_sb[:], res_v)
-            if step == 1:
-                project(0)
-                deal(1)
-            if step == 2:
-                deal(2)
-            if step > 0:
-                project(step)
+            if 0 < step < LISTS:
+                deal(step)
+            project(step)
             if g == LISTS - 1:
                 act = activate(b)
                 hs[b] = new_h()
-                if b < last:
+                if b < last - 1:
                     smooth_scalar(act[:], hs[b][:])
+                elif b < last:
+                    smooth_scalar(act[:, :, 0:P], hs[b][:, 0:P, :])
+                    before = act
             if step == 3 * last - 1:
                 finish(quantise(hs[0][:], BLOCK), 0, BLOCK)
             if step == STEPS - 2:
                 operand[1] = quantise(hs[1][:], BLOCK)
+                smooth_vector(before[:, :, P:BLOCK], hs[last - 1][:, P:BLOCK, :])
         finish(operand[1], BLOCK, BLOCK)
         finish(quantise(hs[2][:], BLOCK), 2 * BLOCK, BLOCK)
-        for i in range(TILES):
-            smooth_vector(act[:, :, P * i : P * (i + 1)], hs[last][:, P * i : P * (i + 1), :])
+        smooth_vector(act[:, :, 0:P], hs[last][:, 0:P, :])
+        smooth_scalar(act[:, :, P:BLOCK], hs[last][:, P:BLOCK, :])
         tail = [quantise(hs[last][:, P * i : P * (i + 1), :], P) for i in range(TILES)]
         for i in range(TILES):
             finish(tail[i], last * BLOCK + P * i, P)

@@ -67,11 +67,10 @@ def tile_list_rvq_silu_res_kernel(
 
         tab_s = keep.tile([P, T // 4], I32, name="tab_s", align_bytes=64)
         nc.gpsimd.memset(tab_s[:], 0)
-        staged = keep.tile([P, LISTS, R // 4], I32, name="staged", align_bytes=64)
+        staged = keep.tile([P, R // 4], I32, name="staged", align_bytes=64)
         for g in range(LISTS):
-            nc.sync.dma_start(staged[0:32, g, :], w_scales[g].bitcast(I32).rearrange("a q n -> q a n"))
-        nc.vector.memset(staged[32:64], 0)
-        nc.vector.memset(staged[64:128], 0)
+            nc.sync.dma_start(staged[g:96:LISTS, :], w_scales[g].bitcast(I32).rearrange("a q n -> q a n"))
+        nc.vector.memset(staged[96:128], 0)
         planes = keep.tile([P, 2, LISTS * R // 4], I32, name="planes", align_bytes=64)
         nc.vector.memset(planes[:], 0)
         moved_all = keep.tile([P, LISTS * J // 4], I32, name="moved_all", align_bytes=64)
@@ -84,7 +83,7 @@ def tile_list_rvq_silu_res_kernel(
 
         rows = tab_scales.bitcast(I32).rearrange("a (q r) n -> r q a n", r=4)
         for r in range(4):
-            nc.sync.dma_start(tab_s[r:P:SECOND, :], rows[r])
+            (nc.scalar, nc.sync)[r % 2].dma_start(tab_s[r:P:SECOND, :], rows[r])
         tab_w = keep.tile([P, T], I32, name="tab_w", align_bytes=64)
         nc.sync.dma_start(tab_w[:], tab_words[0].rearrange("p n t -> p (n t)").bitcast(I32))
         load_weight(0)
@@ -99,11 +98,12 @@ def tile_list_rvq_silu_res_kernel(
                                   w_sb[g][:].bitcast(U32).rearrange("p a (c i t) -> p a c t i", t=4, i=4))
 
         def deal_scales():
-            tile = keep.tile([P, LISTS * R], U8, name="dealt_scales", align_bytes=64)
-            nc.vector.tensor_copy(tile[:].rearrange("p (g t c i) -> p c g t i", g=LISTS, t=4, i=16),
-                                  staged[:].bitcast(U8).rearrange("p g (c i t) -> p c g t i", t=4, i=16))
+            tile = keep.tile([P, R], U8, name="dealt_scales", align_bytes=64)
+            nc.vector.tensor_copy(tile[:].rearrange("p (t c i) -> p c t i", t=4, i=16),
+                                  staged[:].bitcast(U8).rearrange("p (c i t) -> p c t i", t=4, i=16))
             for q in range(4):
-                nc.scalar.dma_start(planes[32 * q : 32 * q + 4], tile[:].bitcast(I32)[8 * q : 8 * q + 8, :])
+                nc.scalar.dma_start(planes[32 * q : 32 * q + 4].rearrange("p a (g n) -> p (a g) n", g=LISTS),
+                                    tile[:].bitcast(I32)[24 * q : 24 * q + 24, :])
 
         picked = {}
         moved = {}
@@ -141,7 +141,8 @@ def tile_list_rvq_silu_res_kernel(
             size = LINK + MAIN + tenants.get(step, 0) + LINK
             tile = shared.tile([P, size], U8, name="parted%d" % step, offset=place[step], align_bytes=64)
             parted = tile[:, LINK : LINK + MAIN].rearrange("p (a n) -> p a n", a=2)
-            nc.vector.tensor_copy(parted.bitcast(U16), words.bitcast(U16).rearrange("p (n d) -> p d n", d=2))
+            nc.vector.tensor_copy(parted.bitcast(U16).rearrange("p d (c i) -> p c d i", i=8),
+                                  words.bitcast(U16).rearrange("p (c i d) -> p c d i", d=2, i=8))
             return parted
 
         acc = {}
@@ -210,7 +211,6 @@ def tile_list_rvq_silu_res_kernel(
         deal_scales()
         gather_scales((0, 1, 2), 0, keep.tile([P, LISTS * HALF], U8, name="picked_first", align_bytes=64), nc.scalar)
         hs = {}
-        operand = {}
         words = gather_words(0)
         deal(0)
         parts[0] = part(0, words)
@@ -251,12 +251,12 @@ def tile_list_rvq_silu_res_kernel(
             if step == 3 * last - 1:
                 finish(quantise(hs[0][:], BLOCK), 0, BLOCK)
             if step == STEPS - 2:
-                operand[1] = quantise(hs[1][:], BLOCK)
+                finish(quantise(hs[1][:], BLOCK), BLOCK, BLOCK)
                 smooth_vector(before[:, :, P:BLOCK], hs[last - 1][:, P:BLOCK, :])
-        finish(operand[1], BLOCK, BLOCK)
-        finish(quantise(hs[2][:], BLOCK), 2 * BLOCK, BLOCK)
+        operand = quantise(hs[2][:], BLOCK)
         smooth_vector(act[:, :, 0:P], hs[last][:, 0:P, :])
         smooth_scalar(act[:, :, P:BLOCK], hs[last][:, P:BLOCK, :])
         tail = [quantise(hs[last][:, P * i : P * (i + 1), :], P) for i in range(TILES)]
+        finish(operand, 2 * BLOCK, BLOCK)
         for i in range(TILES):
             finish(tail[i], last * BLOCK + P * i, P)

@@ -94,7 +94,7 @@ def tile_list_rvq_silu_res_kernel(
 
         def deal(g):
             dealt[g] = keep.tile([P, 2, R], U32, name="dealt%d" % g, align_bytes=64)
-            nc.vector.tensor_copy(dealt[g][:].rearrange("p a (t c i) -> p a c t i", t=4, i=4),
+            (nc.vector, nc.gpsimd, nc.gpsimd)[g].tensor_copy(dealt[g][:].rearrange("p a (t c i) -> p a c t i", t=4, i=4),
                                   w_sb[g][:].bitcast(U32).rearrange("p a (c i t) -> p a c t i", t=4, i=4))
 
         def deal_scales():

@@ -19,14 +19,13 @@ ALU = mybir.AluOpType
 P = 128
 LISTS = 3
 BLOCK = 256
-TILES = BLOCK // P
 BLOCKS = J // BLOCK
-STEPS = LISTS * BLOCKS
-HALF = J // 2
-LAG = 3
-LINK = 64
-MAIN = 4 * BLOCK
 SECOND = 16
+HEAD = 6
+LEAD = 4
+RAW = 8 * R
+LINK = 64
+ZONE = 5 * BLOCK
 
 
 def tile_list_rvq_silu_res_kernel(
@@ -38,27 +37,23 @@ def tile_list_rvq_silu_res_kernel(
     w_scales = (w0_scales, w1_scales, w2_scales)
     res_v = res.rearrange("(h p) j -> p h j", p=P)
     out_v = out.rearrange("(h p) j -> p h j", p=P)
-    last = BLOCKS - 1
 
-    scales_after = {3: 0, 5: 1, 6: 2}
-    tenants = {step - LAG: HALF for step in scales_after}
-    tenants[4] = 2 * J * 4
-    tenants[0] = 0
-    tenants[1] = 3 * N + LINK
-    place = {}
-    end = 0
-    for chain in range(LAG):
-        for step in range(chain, STEPS, LAG):
-            place[step] = end
-            end = end + LINK + MAIN + tenants.get(step, 0)
-        end = end + LINK
-    first_words = end
-    raw_at = {2: first_words + MAIN, 0: first_words + MAIN + 8 * R, 1: first_words + MAIN + 16 * R}
-    place[0] = raw_at[0] + 8 * R - MAIN - 2 * LINK
+    pieces = [(b * BLOCK, BLOCK) for b in range(BLOCKS - 1)] + [(J - BLOCK, P), (J - P, P)]
+    steps = [(n, g) for n in range(len(pieces)) for g in range(LISTS)]
+    raw_at = [ZONE, ZONE + RAW, ZONE + 2 * RAW]
+    zone = {}
+    end = ZONE + 3 * RAW - LINK
+    for step in list(range(LISTS, len(steps), 2)) + [None] + list(range(0, len(steps), 2)) + [None]:
+        zone[step] = end
+        end = end + ZONE
+
+    zone[1] = 0
+
+    def parted_at(step):
+        return zone[step - 1] if step > 0 else end
 
     with ExitStack() as ctx:
         keep = ctx.enter_context(tc.tile_pool(name="keep", bufs=1))
-        ring = ctx.enter_context(tc.tile_pool(name="ring", bufs=2 * BLOCKS))
         shared = ctx.enter_context(tc.tile_pool(name="shared", bufs=1))
         psum = ctx.enter_context(tc.psum_pool(name="psum", bufs=1))
 
@@ -68,195 +63,208 @@ def tile_list_rvq_silu_res_kernel(
         tab_s = keep.tile([P, T // 4], I32, name="tab_s", align_bytes=64)
         nc.gpsimd.memset(tab_s[:], 0)
         staged = keep.tile([P, R // 4], I32, name="staged", align_bytes=64)
-        for g in range(LISTS):
-            nc.sync.dma_start(staged[g:96:LISTS, :], w_scales[g].bitcast(I32).rearrange("a q n -> q a n"))
+
+        def stage(g):
+            rows = staged[g:64:2, :] if g < 2 else staged[64:96, :]
+            nc.sync.dma_start(rows, w_scales[g].bitcast(I32).rearrange("a q n -> q a n"))
+
+        stage(0)
+        stage(1)
         nc.vector.memset(staged[96:128], 0)
-        planes = keep.tile([P, 2, LISTS * R // 4], I32, name="planes", align_bytes=64)
-        nc.vector.memset(planes[:], 0)
+        planes = keep.tile([P, 4, R // 4], I32, name="planes", align_bytes=64)
         moved_all = keep.tile([P, LISTS * J // 4], I32, name="moved_all", align_bytes=64)
-        nc.gpsimd.memset(moved_all[96:128, :], 0)
-
-        w_sb = {g: shared.tile([P, 2, R], I32, name="w%d" % g, offset=raw_at[g], align_bytes=64) for g in range(LISTS)}
-
-        def load_weight(g):
-            nc.sync.dma_start(w_sb[g][:], w_words[g].rearrange("a p n t -> p a (n t)").bitcast(I32))
 
         rows = tab_scales.bitcast(I32).rearrange("a (q r) n -> r q a n", r=4)
         for r in range(4):
-            (nc.scalar, nc.sync)[r % 2].dma_start(tab_s[r:P:SECOND, :], rows[r])
+            nc.sync.dma_start(tab_s[r:P:SECOND, :], rows[r])
         tab_w = keep.tile([P, T], I32, name="tab_w", align_bytes=64)
-        nc.sync.dma_start(tab_w[:], tab_words[0].rearrange("p n t -> p (n t)").bitcast(I32))
+        raw = {}
+
+        def load_weight(g):
+            raw[g] = shared.tile([P, 2, R], I32, name="raw%d" % g, offset=raw_at[g], align_bytes=64)
+            nc.sync.dma_start(raw[g][:], w_words[g].rearrange("a p n t -> p a (n t)").bitcast(I32))
+
         load_weight(0)
+        stage(2)
+        nc.sync.dma_start(tab_w[:], tab_words[0].rearrange("p n t -> p (n t)").bitcast(I32))
         load_weight(1)
         load_weight(2)
+
+        def plane(g, a):
+            return (planes[:, 2 * a + g, :] if g < 2 else late_planes[:, a, :]).bitcast(U8)
 
         dealt = {}
 
         def deal(g):
-            dealt[g] = keep.tile([P, 2, R], U32, name="dealt%d" % g, align_bytes=64)
-            (nc.vector, nc.gpsimd, nc.gpsimd)[g].tensor_copy(dealt[g][:].rearrange("p a (t c i) -> p a c t i", t=4, i=4),
-                                  w_sb[g][:].bitcast(U32).rearrange("p a (c i t) -> p a c t i", t=4, i=4))
+            for a in range(2):
+                dealt[g, a] = keep.tile([P, R], U32, name="dealt%d_%d" % (g, a), align_bytes=64)
+                nc.scalar.copy(dealt[g, a][:].rearrange("p (t c i) -> p c t i", t=4, i=4),
+                               raw[g][:, a, :].bitcast(U32).rearrange("p (c i t) -> p c t i", t=4, i=4))
 
         def deal_scales():
-            tile = keep.tile([P, R], U8, name="dealt_scales", align_bytes=64)
+            tile = shared.tile([P, R], U8, name="dealt_scales", offset=raw_at[2] + RAW, align_bytes=64)
             nc.vector.tensor_copy(tile[:].rearrange("p (t c i) -> p c t i", t=4, i=16),
                                   staged[:].bitcast(U8).rearrange("p (c i t) -> p c t i", t=4, i=16))
+            rows = tile[:].bitcast(I32)
             for q in range(4):
-                nc.scalar.dma_start(planes[32 * q : 32 * q + 4].rearrange("p a (g n) -> p (a g) n", g=LISTS),
-                                    tile[:].bitcast(I32)[24 * q : 24 * q + 24, :])
+                nc.scalar.dma_start(planes[32 * q : 32 * q + 4, :, :], rows[16 * q : 16 * q + 16, :])
+            return rows
 
         picked = {}
-        moved = {}
 
-        def gather_scales(lists, half, tile, queue):
-            at = (half * LISTS + lists[0]) * HALF // 4
-            dst = moved_all[:, at : at + len(lists) * HALF // 4]
-            for n, g in enumerate(lists):
-                first = (g * J + half * HALF) // 16
-                picked[g, half] = tile[:, n * HALF : (n + 1) * HALF]
-                moved[g, half] = dst.bitcast(U8)[:, n * HALF : (n + 1) * HALF]
-                nc.vector.tensor_copy(picked[g, half], tab_s[:].bitcast(U8).indirect(offsets[:, first : first + HALF // 16]))
-            queue.dma_start(dst[0 : P - SECOND, :], tile[:].bitcast(I32)[SECOND:P, :])
+        def gather_scales(k, dst):
+            b, g = divmod(k, LISTS)
+            first = (g * J + b * BLOCK) // 16
+            picked[k] = dst
+            nc.vector.tensor_copy(dst, tab_s[:].bitcast(U8).indirect(offsets[:, first : first + BLOCK // 16]))
+
+        def shift(k, tile, queue):
+            cols = tile.shape[1] // 4
+            queue.dma_start(moved_all[0 : P - SECOND, k * BLOCK // 4 : k * BLOCK // 4 + cols], tile[:].bitcast(I32)[SECOND:P, :])
 
         def gather_words(step):
-            b, g = divmod(step, LISTS)
-            if step == 0:
-                tile = shared.tile([P, BLOCK], U32, name="words0", offset=first_words, align_bytes=64)
-            elif step < LAG:
-                tile = shared.tile([P, BLOCK], U32, name="words%d" % step, offset=raw_at[0] + MAIN * (step - 1), align_bytes=64)
-            elif step == LAG:
-                tile = shared.tile([P, BLOCK], U32, name="words%d" % step, offset=raw_at[1], align_bytes=64)
-            elif step <= LAG + 2:
-                tile = shared.tile([P, BLOCK], U32, name="words%d" % step,
-                                   offset=raw_at[2] + MAIN * (step - LAG), align_bytes=64)
-            else:
-                tile = shared.tile([P, BLOCK], U32, name="words%d" % step,
-                                   offset=place[step - 1 - LAG] + LINK, align_bytes=64)
-            first = (g * J + b * BLOCK) // 16
-            words = tile[:, 0:BLOCK]
-            nc.vector.tensor_copy(words, tab_w[:].bitcast(U32).indirect(offsets[:, first : first + BLOCK // 16]))
+            n, g = steps[step]
+            at, cols = pieces[n]
+            words = shared.tile([P, (ZONE + LINK) // 4], U32, name="words%d" % step, offset=zone[step], align_bytes=64)[:, 0:cols]
+            first = (g * J + at) // 16
+            nc.vector.tensor_copy(words, tab_w[:].bitcast(U32).indirect(offsets[:, first : first + cols // 16]))
             return words
 
         def part(step, words):
-            size = LINK + MAIN + tenants.get(step, 0) + LINK
-            tile = shared.tile([P, size], U8, name="parted%d" % step, offset=place[step], align_bytes=64)
-            parted = tile[:, LINK : LINK + MAIN].rearrange("p (a n) -> p a n", a=2)
-            nc.vector.tensor_copy(parted.bitcast(U16).rearrange("p d (c i) -> p c d i", i=8),
+            cols = words.shape[1]
+            parted = shared.tile([P, 2, 2 * cols], U8, name="parted%d" % step, offset=parted_at(step), align_bytes=64)
+            nc.vector.tensor_copy(parted[:].bitcast(U16).rearrange("p d (c i) -> p c d i", i=8),
                                   words.bitcast(U16).rearrange("p (c i d) -> p c d i", d=2, i=8))
             return parted
 
-        acc = {}
-        parts = {}
+        banks = {}
+        used = []
 
-        def project(step):
-            b, g = divmod(step, LISTS)
-            half, at = divmod(b * BLOCK, HALF)
-            for t in range(4):
-                if g == 0:
-                    acc[b, t] = psum.tile([P, BLOCK], F32, name="acc", tag="bank", bufs=8)
-                for a in range(2):
-                    for i in range(TILES):
-                        nc.tensor.matmul_mx(
-                            out=acc[b, t][:, P * i : P * (i + 1)],
-                            lhsT=dealt[g][:, a, P * t : P * (t + 1)].bitcast(FP8X4),
-                            lhsT_scale=planes[:, a, :].bitcast(U8)[:, g * R + P * t : g * R + P * (t + 1)],
-                            rhs=parts[step][:, a, 2 * P * i : 2 * P * (i + 1)].bitcast(FP4X4),
-                            rhs_scale=(picked, moved)[a][g, half][:, at + P * i : at + P * (i + 1)],
-                            start=(g == 0 and a == 0 and i == 0),
-                            stop=(g == LISTS - 1 and a == 1 and i == TILES - 1),
-                        )
+        def project(step, parted):
+            n, g = steps[step]
+            at, cols = pieces[n]
+            per_bank = 4 * P // cols
+            k = (at // BLOCK) * LISTS + g
+            within = at % BLOCK
+            scales = (picked[k], moved_all[:].bitcast(U8)[:, k * BLOCK : (k + 1) * BLOCK])
+            order = [(a, t) for a in range(2) for t in range(4)]
+            if g == LISTS - 1:
+                order = [(a, t) for u in range(0, 4, per_bank) for a in range(2) for t in range(u, u + per_bank)]
+            for a, t in order:
+                u, v = divmod(t, per_bank)
+                if (n, u) not in banks:
+                    banks[n, u] = psum.tile([P, per_bank, cols], F32, name="acc", tag="bank%d" % len(used))
+                    used.append((n, u))
+                nc.tensor.matmul_mx(
+                    out=banks[n, u][:, v, :],
+                    lhsT=dealt[g, a][:, P * t : P * (t + 1)].bitcast(FP8X4),
+                    lhsT_scale=plane(g, a)[:, P * t : P * (t + 1)],
+                    rhs=parted[:, a, :].bitcast(FP4X4),
+                    rhs_scale=scales[a][:, within : within + cols],
+                    start=(g == 0 and a == 0 and v == 0),
+                    stop=(g == LISTS - 1 and a == 1 and v == per_bank - 1),
+                )
 
-        def activate(b):
-            act = ring.tile([P, 4, BLOCK], F32, name="act", align_bytes=64)
-            for t in range(4):
-                nc.scalar.activation(act[:, t, :], acc[b, t][:], ACT.Silu)
+        def activate(n):
+            cols = pieces[n][1]
+            per_bank = 4 * P // cols
+            act = keep.tile([P, 4, cols], F32, name="act%d" % n, align_bytes=64)
+            for u in range(4 // per_bank):
+                nc.scalar.activation(act[:, u * per_bank : (u + 1) * per_bank, :], banks[n, u][:], ACT.Silu)
             return act
 
-        def smooth_scalar(act, h_cols):
-            flat = ring.tile(list(act.shape), BF16, name="flat", align_bytes=64)
+        def smooth_scalar(n, act):
+            cols = pieces[n][1]
+            flat = keep.tile([P, 4, cols], BF16, name="flat%d" % n, align_bytes=64)
             for t in range(4):
                 nc.scalar.activation(flat[:, t, :], act[:, t, :], ACT.Copy, scale=sm_sb[:, t : t + 1])
-            nc.scalar.copy(h_cols.rearrange("p (c i) t -> p c t i", i=4), flat[:].rearrange("p t (c i) -> p c t i", i=4))
+            h = keep.tile([P, cols, 4], BF16, name="h%d" % n, align_bytes=64)
+            nc.scalar.copy(h[:].rearrange("p (c i) t -> p c t i", i=4), flat[:].rearrange("p t (c i) -> p c t i", i=4))
+            return h
 
-        def smooth_vector(act, h_cols):
-            nc.vector.tensor_tensor(h_cols, act.rearrange("p t j -> p j t"),
-                                    sm_sb[:].unsqueeze(1).to_broadcast([P, P, 4]), ALU.mult)
+        def smooth_vector(n, act):
+            cols = pieces[n][1]
+            h = keep.tile([P, cols, 4], BF16, name="h%d" % n, align_bytes=64)
+            nc.vector.tensor_tensor(h[:].rearrange("p (c i) t -> p c t i", i=4), act[:].rearrange("p t (c i) -> p c t i", i=4),
+                                    sm_sb[:].unsqueeze(1).unsqueeze(3).to_broadcast([P, cols // 4, 4, 4]), ALU.mult)
+            return h
 
-        def quantise(h, cols):
-            codes = ring.tile([P, cols], U32, name="codes", align_bytes=64)
-            scales = ring.tile([P, cols], U8, name="scales", align_bytes=64)
-            nc.vector.quantize_mx(out=codes[:].bitcast(FP8X4), scales=scales[:], in_=h.rearrange("p j t -> p (j t)"))
+        def quantise(n, h):
+            cols = pieces[n][1]
+            codes = keep.tile([P, cols], U32, name="codes%d" % n, align_bytes=64)
+            scales = keep.tile([P, cols], U8, name="scales%d" % n, align_bytes=64)
+            nc.vector.quantize_mx(out=codes[:].bitcast(FP8X4), scales=scales[:], in_=h[:].rearrange("p j t -> p (j t)"))
             return codes, scales
 
-        def finish(operand, first, cols):
+        def second(n, operand):
             codes, scales = operand
-            y = psum.tile([P, 2, cols], F32, name="y", tag="bank", bufs=8)
+            y = psum.tile([P, 2, pieces[n][1]], F32, name="y", tag="bank%d" % n)
             for half in range(2):
                 nc.tensor.matmul_mx(
                     out=y[:, half, :],
                     lhsT=wd_sb[:].bitcast(U8)[:, 2 * P * half : 2 * P * (half + 1)].bitcast(FP4X4),
-                    lhsT_scale=wd_plane.bitcast(U8)[:, P * half : P * (half + 1)],
+                    lhsT_scale=wd_plane[:].bitcast(U8)[:, P * half : P * (half + 1)],
                     rhs=codes[:].bitcast(FP8X4),
                     rhs_scale=scales[:],
                     start=True,
                     stop=True,
                 )
-            result = ring.tile([P, 2, cols], F32, name="result")
-            nc.vector.tensor_tensor(result[:], y[:], res_sb[:, :, first : first + cols], ALU.add)
-            nc.sync.dma_start(out_v[:, :, first : first + cols], result[:])
+            return y
 
-        def new_h():
-            return ring.tile([P, BLOCK, 4], BF16, name="h", align_bytes=64)
+        def finish(n, y):
+            at, cols = pieces[n]
+            result = keep.tile([P, 2, cols], F32, name="result%d" % n)
+            nc.vector.tensor_tensor(result[:], y[:], res_sb[at // BLOCK][:, :, at % BLOCK : at % BLOCK + cols], ALU.add)
+            nc.sync.dma_start(out_v[:, :, at : at + cols], result[:])
 
-        deal_scales()
-        gather_scales((0, 1, 2), 0, keep.tile([P, LISTS * HALF], U8, name="picked_first", align_bytes=64), nc.scalar)
-        hs = {}
-        words = gather_words(0)
-        deal(0)
-        parts[0] = part(0, words)
-        for step in range(STEPS):
-            b, g = divmod(step, LISTS)
-            ahead = gather_words(step + 1) if step + 1 < STEPS else None
-            if step > 0:
-                parts[step] = part(step, words)
-            words = ahead
-            if step in scales_after:
-                tile = shared.tile([P, HALF], U8, name="picked%d" % step,
-                                   offset=raw_at[2] + 3 * MAIN if step == LAG else place[step - LAG] + LINK + MAIN,
-                                   align_bytes=64)
-                gather_scales((scales_after[step],), 1, tile, nc.sync)
-            if step == 1:
-                wd_plane = shared.tile([P, N // 4], I32, name="wd_plane", offset=place[1] + LINK + MAIN, align_bytes=64)[:]
-                nc.gpsimd.memset(wd_plane, 0)
-                sm_sb = shared.tile([P, 4], F32, name="sm_sb", offset=place[1] + LINK + MAIN + 3 * N, align_bytes=64)
+        for b in range(HEAD // LISTS):
+            head = keep.tile([P, LISTS * BLOCK], U8, name="picked_head%d" % b, align_bytes=64)
+            for g in range(LISTS):
+                gather_scales(b * LISTS + g, head[:, g * BLOCK : (g + 1) * BLOCK])
+                if b == 0 and g == 0:
+                    dealt_rows = deal_scales()
+            shift(b * LISTS, head, (nc.scalar, nc.sync)[b])
+
+        acts, hs, ys, res_sb = {}, {}, {}, {}
+        for step, (n, g) in enumerate(steps):
+            words = gather_words(step)
+            k = step + LEAD - 1
+            if HEAD <= k < LISTS * BLOCKS:
+                tile = shared.tile([P, BLOCK], U8, name="picked%d" % k, offset=zone[k - LEAD] + 4 * BLOCK, align_bytes=64)
+                gather_scales(k, tile[:])
+                shift(k, tile, nc.sync)
+            parted = part(step, words)
+            if step < LISTS:
+                deal(step)
+            if step == 0:
+                late_planes = shared.tile([P, 2, R // 4], I32, name="late_planes", offset=raw_at[0] + 8 * N, align_bytes=64)
+                for q in range(4):
+                    nc.sync.dma_start(late_planes[32 * q : 32 * q + 4, :, :], dealt_rows[64 + 8 * q : 64 + 8 * q + 8, :])
+                sm_sb = shared.tile([P, 4], F32, name="sm_sb", offset=raw_at[0] + LINK, align_bytes=64)
                 nc.sync.dma_start(sm_sb[:], sm.rearrange("(p t) -> p t", t=4))
-                wd_sb = shared.tile([P, 2 * N // 4], I32, name="wd_sb", offset=place[1] + LINK + MAIN + N, align_bytes=64)
+                wd_sb = shared.tile([P, 2 * N // 4], I32, name="wd_sb", offset=raw_at[0] + N, align_bytes=64)
                 nc.sync.dma_start(wd_sb[:], wd_words[0].bitcast(I32))
+                wd_plane = shared.tile([P, N // 4], I32, name="wd_plane", offset=raw_at[0] + 4 * N, align_bytes=64)
                 for q in range(4):
                     nc.sync.dma_start(wd_plane[32 * q : 32 * q + 4, :], wd_scales.bitcast(I32)[0, 4 * q : 4 * q + 4, :])
-            if step == 4 + LAG:
-                res_sb = shared.tile([P, 2, J], F32, name="res_sb", offset=place[4] + LINK + MAIN, align_bytes=64)
-                nc.sync.dma_start(res_sb[:], res_v)
-            if 0 < step < LISTS:
-                deal(step)
-            project(step)
+            project(step, parted)
+            if 3 <= step < 3 + BLOCKS:
+                b = step - 3
+                res_sb[b] = shared.tile([P, 2, BLOCK], F32, name="res%d" % b, offset=raw_at[1] + 8 * BLOCK * b, align_bytes=64)
+                nc.sync.dma_start(res_sb[b][:], res_v[:, :, b * BLOCK : (b + 1) * BLOCK])
             if g == LISTS - 1:
-                act = activate(b)
-                hs[b] = new_h()
-                if b < last - 1:
-                    smooth_scalar(act[:], hs[b][:])
-                elif b < last:
-                    smooth_scalar(act[:, :, 0:P], hs[b][:, 0:P, :])
-                    before = act
-            if step == 3 * last - 1:
-                finish(quantise(hs[0][:], BLOCK), 0, BLOCK)
-            if step == STEPS - 2:
-                finish(quantise(hs[1][:], BLOCK), BLOCK, BLOCK)
-                smooth_vector(before[:, :, P:BLOCK], hs[last - 1][:, P:BLOCK, :])
-        operand = quantise(hs[2][:], BLOCK)
-        smooth_vector(act[:, :, 0:P], hs[last][:, 0:P, :])
-        smooth_scalar(act[:, :, P:BLOCK], hs[last][:, P:BLOCK, :])
-        tail = [quantise(hs[last][:, P * i : P * (i + 1), :], P) for i in range(TILES)]
-        finish(operand, 2 * BLOCK, BLOCK)
-        for i in range(TILES):
-            finish(tail[i], last * BLOCK + P * i, P)
+                acts[n] = activate(n)
+                if n < BLOCKS - 1:
+                    hs[n] = smooth_scalar(n, acts[n])
+            if step == LISTS * BLOCKS - 1:
+                for m in range(2):
+                    ys[m] = second(m, quantise(m, hs[m]))
+        for m in range(2):
+            finish(m, ys[m])
+        ys[2] = second(2, quantise(2, hs[2]))
+        for m in (3, 4):
+            hs[m] = smooth_vector(m, acts[m])
+        for m in (3, 4):
+            ys[m] = second(m, quantise(m, hs[m]))
+        for m in (2, 3, 4):
+            finish(m, ys[m])

@@ -21,11 +21,12 @@ LISTS = 3
 BLOCK = 256
 BLOCKS = J // BLOCK
 SECOND = 16
-HEAD = 6
+HEAD = 4
 LEAD = 4
 RAW = 8 * R
 LINK = 64
-ZONE = 5 * BLOCK
+HALF = J // 2
+ZONE = 4 * BLOCK + HALF
 
 
 def tile_list_rvq_silu_res_kernel(
@@ -39,7 +40,9 @@ def tile_list_rvq_silu_res_kernel(
     out_v = out.rearrange("(h p) j -> p h j", p=P)
 
     pieces = [(b * BLOCK, BLOCK) for b in range(BLOCKS - 1)] + [(J - BLOCK, P), (J - P, P)]
-    steps = [(n, g) for n in range(len(pieces)) for g in range(LISTS)]
+    steps = [(b, g) for b in range(BLOCKS) for g in range(LISTS)]
+    pieces_of = {b: [n for n in range(len(pieces)) if pieces[n][0] // BLOCK == b] for b in range(BLOCKS)}
+    scales_in = {2: (0, HALF, HALF), 3: (1, HALF, HALF), 5: (2, HALF, BLOCK), 9: (2, HALF + BLOCK, BLOCK)}
     raw_at = [ZONE, ZONE + RAW, ZONE + 2 * RAW]
     zone = {}
     end = ZONE + 3 * RAW - LINK
@@ -47,9 +50,15 @@ def tile_list_rvq_silu_res_kernel(
         zone[step] = end
         end = end + ZONE
 
-    zone[1] = 0
+    zone[1] = end
+    end = end + 2 * ZONE
+
+    h_at = [end + ZONE + 8 * BLOCK * n for n in range(len(pieces))]
+    after_h = {8: 0}
 
     def parted_at(step):
+        if step in after_h:
+            return h_at[after_h[step]]
         return zone[step - 1] if step > 0 else end
 
     with ExitStack() as ctx:
@@ -62,7 +71,7 @@ def tile_list_rvq_silu_res_kernel(
 
         tab_s = keep.tile([P, T // 4], I32, name="tab_s", align_bytes=64)
         nc.gpsimd.memset(tab_s[:], 0)
-        staged = keep.tile([P, R // 4], I32, name="staged", align_bytes=64)
+        staged = shared.tile([P, R // 4], I32, name="staged", offset=raw_at[2] - R // 2, align_bytes=64)
 
         def stage(g):
             rows = staged[g:64:2, :] if g < 2 else staged[64:96, :]
@@ -70,9 +79,9 @@ def tile_list_rvq_silu_res_kernel(
 
         stage(0)
         stage(1)
+        stage(2)
         nc.vector.memset(staged[96:128], 0)
         planes = keep.tile([P, 4, R // 4], I32, name="planes", align_bytes=64)
-        moved_all = keep.tile([P, LISTS * J // 4], I32, name="moved_all", align_bytes=64)
 
         rows = tab_scales.bitcast(I32).rearrange("a (q r) n -> r q a n", r=4)
         for r in range(4):
@@ -84,11 +93,8 @@ def tile_list_rvq_silu_res_kernel(
             raw[g] = shared.tile([P, 2, R], I32, name="raw%d" % g, offset=raw_at[g], align_bytes=64)
             nc.sync.dma_start(raw[g][:], w_words[g].rearrange("a p n t -> p a (n t)").bitcast(I32))
 
-        load_weight(0)
-        stage(2)
         nc.sync.dma_start(tab_w[:], tab_words[0].rearrange("p n t -> p (n t)").bitcast(I32))
-        load_weight(1)
-        load_weight(2)
+        load_weight(0)
 
         def plane(g, a):
             return (planes[:, 2 * a + g, :] if g < 2 else late_planes[:, a, :]).bitcast(U8)
@@ -107,24 +113,29 @@ def tile_list_rvq_silu_res_kernel(
                                   staged[:].bitcast(U8).rearrange("p (c i t) -> p c t i", t=4, i=16))
             rows = tile[:].bitcast(I32)
             for q in range(4):
-                nc.scalar.dma_start(planes[32 * q : 32 * q + 4, :, :], rows[16 * q : 16 * q + 16, :])
+                nc.sync.dma_start(planes[32 * q : 32 * q + 4, :, :], rows[16 * q : 16 * q + 16, :])
+            load_weight(1)
+            load_weight(2)
             return rows
 
         picked = {}
+        moved = {}
 
-        def gather_scales(k, dst):
-            b, g = divmod(k, LISTS)
-            first = (g * J + b * BLOCK) // 16
-            picked[k] = dst
-            nc.vector.tensor_copy(dst, tab_s[:].bitcast(U8).indirect(offsets[:, first : first + BLOCK // 16]))
-
-        def shift(k, tile, queue):
-            cols = tile.shape[1] // 4
-            queue.dma_start(moved_all[0 : P - SECOND, k * BLOCK // 4 : k * BLOCK // 4 + cols], tile[:].bitcast(I32)[SECOND:P, :])
+        def gather_scales(runs, tile, dst):
+            at = 0
+            for g, first, cols in runs:
+                for b in range(first // BLOCK, (first + cols) // BLOCK):
+                    own = slice(at + b * BLOCK - first, at + (b + 1) * BLOCK - first)
+                    picked[g, b] = tile[:, own]
+                    moved[g, b] = dst[:].bitcast(U8)[:, own]
+                col = (g * J + first) // 16
+                nc.vector.tensor_copy(tile[:, at : at + cols], tab_s[:].bitcast(U8).indirect(offsets[:, col : col + cols // 16]))
+                at = at + cols
+            nc.sync.dma_start(dst[0 : P - SECOND, :], tile[:].bitcast(I32)[SECOND:P, :])
 
         def gather_words(step):
-            n, g = steps[step]
-            at, cols = pieces[n]
+            b, g = steps[step]
+            at, cols = b * BLOCK, BLOCK
             words = shared.tile([P, (ZONE + LINK) // 4], U32, name="words%d" % step, offset=zone[step], align_bytes=64)[:, 0:cols]
             first = (g * J + at) // 16
             nc.vector.tensor_copy(words, tab_w[:].bitcast(U32).indirect(offsets[:, first : first + cols // 16]))
@@ -140,14 +151,12 @@ def tile_list_rvq_silu_res_kernel(
         banks = {}
         used = []
 
-        def project(step, parted):
-            n, g = steps[step]
+        def project(n, g, parted, passes):
             at, cols = pieces[n]
             per_bank = 4 * P // cols
-            k = (at // BLOCK) * LISTS + g
             within = at % BLOCK
-            scales = (picked[k], moved_all[:].bitcast(U8)[:, k * BLOCK : (k + 1) * BLOCK])
-            order = [(a, t) for a in range(2) for t in range(4)]
+            scales = (picked[g, at // BLOCK], moved[g, at // BLOCK])
+            order = [(a, t) for a in passes for t in range(4)]
             if g == LISTS - 1:
                 order = [(a, t) for u in range(0, 4, per_bank) for a in range(2) for t in range(u, u + per_bank)]
             for a, t in order:
@@ -159,7 +168,7 @@ def tile_list_rvq_silu_res_kernel(
                     out=banks[n, u][:, v, :],
                     lhsT=dealt[g, a][:, P * t : P * (t + 1)].bitcast(FP8X4),
                     lhsT_scale=plane(g, a)[:, P * t : P * (t + 1)],
-                    rhs=parted[:, a, :].bitcast(FP4X4),
+                    rhs=parted[:, a, 2 * within : 2 * (within + cols)].bitcast(FP4X4),
                     rhs_scale=scales[a][:, within : within + cols],
                     start=(g == 0 and a == 0 and v == 0),
                     stop=(g == LISTS - 1 and a == 1 and v == per_bank - 1),
@@ -173,21 +182,15 @@ def tile_list_rvq_silu_res_kernel(
                 nc.scalar.activation(act[:, u * per_bank : (u + 1) * per_bank, :], banks[n, u][:], ACT.Silu)
             return act
 
-        def smooth_scalar(n, act):
-            cols = pieces[n][1]
-            flat = keep.tile([P, 4, cols], BF16, name="flat%d" % n, align_bytes=64)
+        def smooth_scalar(n, act, h):
+            flat = keep.tile(list(act.shape), BF16, name="flat%d" % n, align_bytes=64)
             for t in range(4):
                 nc.scalar.activation(flat[:, t, :], act[:, t, :], ACT.Copy, scale=sm_sb[:, t : t + 1])
-            h = keep.tile([P, cols, 4], BF16, name="h%d" % n, align_bytes=64)
-            nc.scalar.copy(h[:].rearrange("p (c i) t -> p c t i", i=4), flat[:].rearrange("p t (c i) -> p c t i", i=4))
-            return h
+            nc.scalar.copy(h.rearrange("p (c i) t -> p c t i", i=4), flat[:].rearrange("p t (c i) -> p c t i", i=4))
 
-        def smooth_vector(n, act):
-            cols = pieces[n][1]
-            h = keep.tile([P, cols, 4], BF16, name="h%d" % n, align_bytes=64)
-            nc.vector.tensor_tensor(h[:].rearrange("p (c i) t -> p c t i", i=4), act[:].rearrange("p t (c i) -> p c t i", i=4),
-                                    sm_sb[:].unsqueeze(1).unsqueeze(3).to_broadcast([P, cols // 4, 4, 4]), ALU.mult)
-            return h
+        def smooth_vector(act, h):
+            nc.vector.tensor_tensor(h.rearrange("p (c i) t -> p c t i", i=4), act.rearrange("p t (c i) -> p c t i", i=4),
+                                    sm_sb[:].unsqueeze(1).unsqueeze(3).to_broadcast([P, P // 4, 4, 4]), ALU.mult)
 
         def quantise(n, h):
             cols = pieces[n][1]
@@ -217,27 +220,29 @@ def tile_list_rvq_silu_res_kernel(
             nc.vector.tensor_tensor(result[:], y[:], res_sb[at // BLOCK][:, :, at % BLOCK : at % BLOCK + cols], ALU.add)
             nc.sync.dma_start(out_v[:, :, at : at + cols], result[:])
 
-        for b in range(HEAD // LISTS):
-            head = keep.tile([P, LISTS * BLOCK], U8, name="picked_head%d" % b, align_bytes=64)
-            for g in range(LISTS):
-                gather_scales(b * LISTS + g, head[:, g * BLOCK : (g + 1) * BLOCK])
-                if b == 0 and g == 0:
-                    dealt_rows = deal_scales()
-            shift(b * LISTS, head, (nc.scalar, nc.sync)[b])
+        dealt_rows = deal_scales()
+        gather_scales([(g, 0, HALF) for g in range(LISTS)], keep.tile([P, LISTS * HALF], U8, name="picked_head", align_bytes=64),
+                      keep.tile([P, LISTS * HALF // 4], I32, name="moved_head", align_bytes=64))
 
+        parts = {}
         acts, hs, ys, res_sb = {}, {}, {}, {}
-        for step, (n, g) in enumerate(steps):
+        for step, (block, g) in enumerate(steps):
             words = gather_words(step)
-            k = step + LEAD - 1
-            if HEAD <= k < LISTS * BLOCKS:
-                tile = shared.tile([P, BLOCK], U8, name="picked%d" % k, offset=zone[k - LEAD] + 4 * BLOCK, align_bytes=64)
-                gather_scales(k, tile[:])
-                shift(k, tile, nc.sync)
+            if step in scales_in:
+                run = scales_in[step]
+                tile = shared.tile([P, run[2]], U8, name="picked%d" % step, offset=zone[step - 1] + 4 * BLOCK, align_bytes=64)
+                dst = shared.tile([P, run[2] // 4], I32, name="moved%d" % step,
+                                  offset=raw_at[0] + 9 * N + run[0] * HALF + run[1] - HALF, align_bytes=64)
+                gather_scales([run], tile, dst)
+            if step in after_h:
+                operand = quantise(after_h[step], hs[after_h[step]])
             parted = part(step, words)
+            if step in after_h:
+                ys[after_h[step]] = second(after_h[step], operand)
             if step < LISTS:
                 deal(step)
             if step == 0:
-                late_planes = shared.tile([P, 2, R // 4], I32, name="late_planes", offset=raw_at[0] + 8 * N, align_bytes=64)
+                late_planes = shared.tile([P, 2, R // 4], I32, name="late_planes", offset=raw_at[0] + 5 * N, align_bytes=64)
                 for q in range(4):
                     nc.sync.dma_start(late_planes[32 * q : 32 * q + 4, :, :], dealt_rows[64 + 8 * q : 64 + 8 * q + 8, :])
                 sm_sb = shared.tile([P, 4], F32, name="sm_sb", offset=raw_at[0] + LINK, align_bytes=64)
@@ -247,24 +252,29 @@ def tile_list_rvq_silu_res_kernel(
                 wd_plane = shared.tile([P, N // 4], I32, name="wd_plane", offset=raw_at[0] + 4 * N, align_bytes=64)
                 for q in range(4):
                     nc.sync.dma_start(wd_plane[32 * q : 32 * q + 4, :], wd_scales.bitcast(I32)[0, 4 * q : 4 * q + 4, :])
-            project(step, parted)
+            for n in pieces_of[block]:
+                parts[step] = parted
+                project(n, g, parted, (0,) if step < 2 else (0, 1))
+                if step == 1:
+                    for early in range(2):
+                        project(0, early, parts[early], (1,))
+                if g == LISTS - 1:
+                    acts[n] = activate(n)
+                    hs[n] = shared.tile([P, pieces[n][1], 4], BF16, name="h%d" % n, offset=h_at[n], align_bytes=64)
+                    if n < BLOCKS - 2:
+                        smooth_scalar(n, acts[n][:], hs[n][:])
+                    elif n < BLOCKS - 1:
+                        smooth_scalar(n, acts[n][:, :, 0:P], hs[n][:, 0:P, :])
             if 3 <= step < 3 + BLOCKS:
                 b = step - 3
                 res_sb[b] = shared.tile([P, 2, BLOCK], F32, name="res%d" % b, offset=raw_at[1] + 8 * BLOCK * b, align_bytes=64)
                 nc.sync.dma_start(res_sb[b][:], res_v[:, :, b * BLOCK : (b + 1) * BLOCK])
-            if g == LISTS - 1:
-                acts[n] = activate(n)
-                if n < BLOCKS - 1:
-                    hs[n] = smooth_scalar(n, acts[n])
-            if step == LISTS * BLOCKS - 1:
-                for m in range(2):
-                    ys[m] = second(m, quantise(m, hs[m]))
-        for m in range(2):
-            finish(m, ys[m])
+        ys[1] = second(1, quantise(1, hs[1]))
+        smooth_vector(acts[2][:, :, P:BLOCK], hs[2][:, P:BLOCK, :])
         ys[2] = second(2, quantise(2, hs[2]))
         for m in (3, 4):
-            hs[m] = smooth_vector(m, acts[m])
+            smooth_vector(acts[m][:], hs[m][:])
         for m in (3, 4):
             ys[m] = second(m, quantise(m, hs[m]))
-        for m in (2, 3, 4):
+        for m in range(len(pieces)):
             finish(m, ys[m])

@@ -42,7 +42,7 @@ def tile_list_rvq_silu_res_kernel(
     pieces = [(b * BLOCK, BLOCK) for b in range(BLOCKS - 1)] + [(J - BLOCK, P), (J - P, P)]
     steps = [(b, g) for b in range(BLOCKS) for g in range(LISTS)]
     pieces_of = {b: [n for n in range(len(pieces)) if pieces[n][0] // BLOCK == b] for b in range(BLOCKS)}
-    scales_in = {2: (0, HALF, HALF), 3: (1, HALF, HALF), 5: (2, HALF, BLOCK), 9: (2, HALF + BLOCK, BLOCK)}
+    scales_in = {2: (0, HALF, HALF), 3: (1, HALF, HALF), 10: (2, HALF + BLOCK, BLOCK)}
     raw_at = [ZONE, ZONE + RAW, ZONE + 2 * RAW]
     zone = {}
     end = ZONE + 3 * RAW - LINK
@@ -54,11 +54,12 @@ def tile_list_rvq_silu_res_kernel(
     end = end + 2 * ZONE
 
     h_at = [end + ZONE + 8 * BLOCK * n for n in range(len(pieces))]
-    after_h = {8: 0}
+
+    result_at = {0: zone[len(steps) - 1], 2: h_at[3]}
 
     def parted_at(step):
-        if step in after_h:
-            return h_at[after_h[step]]
+        if step == len(steps) - 1:
+            return h_at[1] - LINK
         return zone[step - 1] if step > 0 else end
 
     with ExitStack() as ctx:
@@ -188,8 +189,8 @@ def tile_list_rvq_silu_res_kernel(
                 nc.scalar.activation(flat[:, t, :], act[:, t, :], ACT.Copy, scale=sm_sb[:, t : t + 1])
             nc.scalar.copy(h.rearrange("p (c i) t -> p c t i", i=4), flat[:].rearrange("p t (c i) -> p c t i", i=4))
 
-        def smooth_vector(act, h):
-            nc.vector.tensor_tensor(h.rearrange("p (c i) t -> p c t i", i=4), act.rearrange("p t (c i) -> p c t i", i=4),
+        def smooth_vector(act, h, engine):
+            engine.tensor_tensor(h.rearrange("p (c i) t -> p c t i", i=4), act.rearrange("p t (c i) -> p c t i", i=4),
                                     sm_sb[:].unsqueeze(1).unsqueeze(3).to_broadcast([P, P // 4, 4, 4]), ALU.mult)
 
         def quantise(n, h):
@@ -216,13 +217,17 @@ def tile_list_rvq_silu_res_kernel(
 
         def finish(n, y):
             at, cols = pieces[n]
-            result = keep.tile([P, 2, cols], F32, name="result%d" % n)
+            if n in result_at:
+                result = shared.tile([P, 2, cols], F32, name="result%d" % n, offset=result_at[n], align_bytes=64)
+            else:
+                result = keep.tile([P, 2, cols], F32, name="result%d" % n)
             nc.vector.tensor_tensor(result[:], y[:], res_sb[at // BLOCK][:, :, at % BLOCK : at % BLOCK + cols], ALU.add)
             nc.sync.dma_start(out_v[:, :, at : at + cols], result[:])
 
         dealt_rows = deal_scales()
-        gather_scales([(g, 0, HALF) for g in range(LISTS)], keep.tile([P, LISTS * HALF], U8, name="picked_head", align_bytes=64),
-                      keep.tile([P, LISTS * HALF // 4], I32, name="moved_head", align_bytes=64))
+        gather_scales([(0, 0, HALF), (1, 0, HALF), (2, 0, HALF + BLOCK)],
+                      keep.tile([P, LISTS * HALF + BLOCK], U8, name="picked_head", align_bytes=64),
+                      keep.tile([P, (LISTS * HALF + BLOCK) // 4], I32, name="moved_head", align_bytes=64))
 
         parts = {}
         acts, hs, ys, res_sb = {}, {}, {}, {}
@@ -234,11 +239,10 @@ def tile_list_rvq_silu_res_kernel(
                 dst = shared.tile([P, run[2] // 4], I32, name="moved%d" % step,
                                   offset=raw_at[0] + 9 * N + run[0] * HALF + run[1] - HALF, align_bytes=64)
                 gather_scales([run], tile, dst)
-            if step in after_h:
-                operand = quantise(after_h[step], hs[after_h[step]])
+            if step == len(steps) - 1:
+                for m in range(2):
+                    ys[m] = second(m, quantise(m, hs[m]))
             parted = part(step, words)
-            if step in after_h:
-                ys[after_h[step]] = second(after_h[step], operand)
             if step < LISTS:
                 deal(step)
             if step == 0:
@@ -265,15 +269,14 @@ def tile_list_rvq_silu_res_kernel(
                         smooth_scalar(n, acts[n][:], hs[n][:])
                     elif n < BLOCKS - 1:
                         smooth_scalar(n, acts[n][:, :, 0:P], hs[n][:, 0:P, :])
+                        smooth_vector(acts[n][:, :, P:BLOCK], hs[n][:, P:BLOCK, :], nc.gpsimd)
             if 3 <= step < 3 + BLOCKS:
                 b = step - 3
                 res_sb[b] = shared.tile([P, 2, BLOCK], F32, name="res%d" % b, offset=raw_at[1] + 8 * BLOCK * b, align_bytes=64)
                 nc.sync.dma_start(res_sb[b][:], res_v[:, :, b * BLOCK : (b + 1) * BLOCK])
-        ys[1] = second(1, quantise(1, hs[1]))
-        smooth_vector(acts[2][:, :, P:BLOCK], hs[2][:, P:BLOCK, :])
         ys[2] = second(2, quantise(2, hs[2]))
         for m in (3, 4):
-            smooth_vector(acts[m][:], hs[m][:])
+            smooth_vector(acts[m][:], hs[m][:], nc.vector)
         for m in (3, 4):
             ys[m] = second(m, quantise(m, hs[m]))
         for m in range(len(pieces)):

from contextlib import ExitStack

import concourse.mybir as mybir

K, R, N, T, J = 1024, 512, 256, 2048, 1024
FLOPS = 2 * (3 * K * R * J + R * N * J)

F32 = mybir.dt.float32
BF16 = mybir.dt.bfloat16
I32 = mybir.dt.int32
U32 = mybir.dt.uint32
U16 = mybir.dt.uint16
U8 = mybir.dt.uint8
FP8X4 = mybir.dt.float8_e4m3fn_x4
FP4X4 = mybir.dt.float4_e2m1fn_x4
ACT = mybir.ActivationFunctionType
ALU = mybir.AluOpType

P = 128
LISTS = 3
BLOCK = 256
BLOCKS = J // BLOCK
SECOND = 16
HEAD = 4
LEAD = 4
RAW = 8 * R
LINK = 64
HALF = J // 2
ZONE = 4 * BLOCK + HALF


def tile_list_rvq_silu_res_kernel(
    tc, tab_words, tab_scales, w0_words, w0_scales, w1_words, w1_scales, w2_words, w2_scales,
    sm, wd_words, wd_scales, res, offs, out,
):
    nc = tc.nc
    w_words = (w0_words, w1_words, w2_words)
    w_scales = (w0_scales, w1_scales, w2_scales)
    res_v = res.rearrange("(h p) j -> p h j", p=P)
    out_v = out.rearrange("(h p) j -> p h j", p=P)

    pieces = [(b * BLOCK, BLOCK) for b in range(BLOCKS - 1)] + [(J - BLOCK, P), (J - P, P)]
    steps = [(b, g) for b in range(BLOCKS) for g in range(LISTS)]
    pieces_of = {b: [n for n in range(len(pieces)) if pieces[n][0] // BLOCK == b] for b in range(BLOCKS)}
    scales_in = {2: (0, HALF, HALF), 3: (1, HALF, HALF), 10: (2, HALF + BLOCK, BLOCK)}
    raw_at = [ZONE, ZONE + RAW, ZONE + 2 * RAW]
    zone = {}
    end = ZONE + 3 * RAW - LINK
    for step in list(range(LISTS, len(steps), 2)) + [None] + list(range(0, len(steps), 2)) + [None]:
        zone[step] = end
        end = end + ZONE

    zone[1] = end
    end = end + 2 * ZONE

    h_at = [end + ZONE + 8 * BLOCK * n for n in range(len(pieces))]

    result_at = {0: zone[len(steps) - 1], 2: h_at[3]}

    def parted_at(step):
        if step == len(steps) - 1:
            return h_at[1] - LINK
        return zone[step - 1] if step > 0 else end

    with ExitStack() as ctx:
        keep = ctx.enter_context(tc.tile_pool(name="keep", bufs=1))
        shared = ctx.enter_context(tc.tile_pool(name="shared", bufs=1))
        psum = ctx.enter_context(tc.psum_pool(name="psum", bufs=1))

        offsets = keep.tile([P, LISTS * J // 16], U16, name="offsets")
        nc.sync.dma_start(offsets[:], offs)

        tab_s = keep.tile([P, T // 4], I32, name="tab_s", align_bytes=64)
        nc.gpsimd.memset(tab_s[:], 0)
        staged = shared.tile([P, R // 4], I32, name="staged", offset=raw_at[2] - R // 2, align_bytes=64)

        def stage(g):
            rows = staged[g:64:2, :] if g < 2 else staged[64:96, :]
            nc.sync.dma_start(rows, w_scales[g].bitcast(I32).rearrange("a q n -> q a n"))

        stage(0)
        stage(1)
        stage(2)
        nc.vector.memset(staged[96:128], 0)
        planes = keep.tile([P, 4, R // 4], I32, name="planes", align_bytes=64)

        rows = tab_scales.bitcast(I32).rearrange("a (q r) n -> r q a n", r=4)
        for r in range(4):
            nc.sync.dma_start(tab_s[r:P:SECOND, :], rows[r])
        tab_w = keep.tile([P, T], I32, name="tab_w", align_bytes=64)
        raw = {}

        def load_weight(g):
            raw[g] = shared.tile([P, 2, R], I32, name="raw%d" % g, offset=raw_at[g], align_bytes=64)
            nc.sync.dma_start(raw[g][:], w_words[g].rearrange("a p n t -> p a (n t)").bitcast(I32))

        nc.sync.dma_start(tab_w[:], tab_words[0].rearrange("p n t -> p (n t)").bitcast(I32))
        load_weight(0)

        def plane(g, a):
            return (planes[:, 2 * a + g, :] if g < 2 else late_planes[:, a, :]).bitcast(U8)

        dealt = {}

        def deal(g):
            for a in range(2):
                dealt[g, a] = keep.tile([P, R], U32, name="dealt%d_%d" % (g, a), align_bytes=64)
                nc.scalar.copy(dealt[g, a][:].rearrange("p (t c i) -> p c t i", t=4, i=4),
                               raw[g][:, a, :].bitcast(U32).rearrange("p (c i t) -> p c t i", t=4, i=4))

        def deal_scales():
            tile = shared.tile([P, R], U8, name="dealt_scales", offset=raw_at[2] + RAW, align_bytes=64)
            nc.vector.tensor_copy(tile[:].rearrange("p (t c i) -> p c t i", t=4, i=16),
                                  staged[:].bitcast(U8).rearrange("p (c i t) -> p c t i", t=4, i=16))
            rows = tile[:].bitcast(I32)
            for q in range(4):
                nc.sync.dma_start(planes[32 * q : 32 * q + 4, :, :], rows[16 * q : 16 * q + 16, :])
            load_weight(1)
            load_weight(2)
            return rows

        picked = {}
        moved = {}

        def gather_scales(runs, tile, dst):
            at = 0
            for g, first, cols in runs:
                for b in range(first // BLOCK, (first + cols) // BLOCK):
                    own = slice(at + b * BLOCK - first, at + (b + 1) * BLOCK - first)
                    picked[g, b] = tile[:, own]
                    moved[g, b] = dst[:].bitcast(U8)[:, own]
                col = (g * J + first) // 16
                nc.vector.tensor_copy(tile[:, at : at + cols], tab_s[:].bitcast(U8).indirect(offsets[:, col : col + cols // 16]))
                at = at + cols
            nc.sync.dma_start(dst[0 : P - SECOND, :], tile[:].bitcast(I32)[SECOND:P, :])

        def gather_words(step):
            b, g = steps[step]
            at, cols = b * BLOCK, BLOCK
            words = shared.tile([P, (ZONE + LINK) // 4], U32, name="words%d" % step, offset=zone[step], align_bytes=64)[:, 0:cols]
            first = (g * J + at) // 16
            nc.vector.tensor_copy(words, tab_w[:].bitcast(U32).indirect(offsets[:, first : first + cols // 16]))
            return words

        def part(step, words):
            cols = words.shape[1]
            parted = shared.tile([P, 2, 2 * cols], U8, name="parted%d" % step, offset=parted_at(step), align_bytes=64)
            nc.vector.tensor_copy(parted[:].bitcast(U16).rearrange("p d (c i) -> p c d i", i=8),
                                  words.bitcast(U16).rearrange("p (c i d) -> p c d i", d=2, i=8))
            return parted

        banks = {}
        used = []

        def project(n, g, parted, passes):
            at, cols = pieces[n]
            per_bank = 4 * P // cols
            within = at % BLOCK
            scales = (picked[g, at // BLOCK], moved[g, at // BLOCK])
            order = [(a, t) for a in passes for t in range(4)]
            if g == LISTS - 1:
                order = [(a, t) for u in range(0, 4, per_bank) for a in range(2) for t in range(u, u + per_bank)]
            for a, t in order:
                u, v = divmod(t, per_bank)
                if (n, u) not in banks:
                    banks[n, u] = psum.tile([P, per_bank, cols], F32, name="acc", tag="bank%d" % len(used))
                    used.append((n, u))
                nc.tensor.matmul_mx(
                    out=banks[n, u][:, v, :],
                    lhsT=dealt[g, a][:, P * t : P * (t + 1)].bitcast(FP8X4),
                    lhsT_scale=plane(g, a)[:, P * t : P * (t + 1)],
                    rhs=parted[:, a, 2 * within : 2 * (within + cols)].bitcast(FP4X4),
                    rhs_scale=scales[a][:, within : within + cols],
                    start=(g == 0 and a == 0 and v == 0),
                    stop=(g == LISTS - 1 and a == 1 and v == per_bank - 1),
                )

        def activate(n):
            cols = pieces[n][1]
            per_bank = 4 * P // cols
            act = keep.tile([P, 4, cols], F32, name="act%d" % n, align_bytes=64)
            for u in range(4 // per_bank):
                nc.scalar.activation(act[:, u * per_bank : (u + 1) * per_bank, :], banks[n, u][:], ACT.Silu)
            return act

        def smooth_scalar(n, act, h):
            flat = keep.tile(list(act.shape), BF16, name="flat%d" % n, align_bytes=64)
            for t in range(4):
                nc.scalar.activation(flat[:, t, :], act[:, t, :], ACT.Copy, scale=sm_sb[:, t : t + 1])
            nc.scalar.copy(h.rearrange("p (c i) t -> p c t i", i=4), flat[:].rearrange("p t (c i) -> p c t i", i=4))

        def smooth_vector(act, h, engine):
            engine.tensor_tensor(h.rearrange("p (c i) t -> p c t i", i=4), act.rearrange("p t (c i) -> p c t i", i=4),
                                    sm_sb[:].unsqueeze(1).unsqueeze(3).to_broadcast([P, P // 4, 4, 4]), ALU.mult)

        def quantise(n, h):
            cols = pieces[n][1]
            codes = keep.tile([P, cols], U32, name="codes%d" % n, align_bytes=64)
            scales = keep.tile([P, cols], U8, name="scales%d" % n, align_bytes=64)
            nc.vector.quantize_mx(out=codes[:].bitcast(FP8X4), scales=scales[:], in_=h[:].rearrange("p j t -> p (j t)"))
            return codes, scales

        def second(n, operand):
            codes, scales = operand
            y = psum.tile([P, 2, pieces[n][1]], F32, name="y", tag="bank%d" % n)
            for half in range(2):
                nc.tensor.matmul_mx(
                    out=y[:, half, :],
                    lhsT=wd_sb[:].bitcast(U8)[:, 2 * P * half : 2 * P * (half + 1)].bitcast(FP4X4),
                    lhsT_scale=wd_plane[:].bitcast(U8)[:, P * half : P * (half + 1)],
                    rhs=codes[:].bitcast(FP8X4),
                    rhs_scale=scales[:],
                    start=True,
                    stop=True,
                )
            return y

        def finish(n, y):
            at, cols = pieces[n]
            if n in result_at:
                result = shared.tile([P, 2, cols], F32, name="result%d" % n, offset=result_at[n], align_bytes=64)
            else:
                result = keep.tile([P, 2, cols], F32, name="result%d" % n)
            nc.vector.tensor_tensor(result[:], y[:], res_sb[at // BLOCK][:, :, at % BLOCK : at % BLOCK + cols], ALU.add)
            nc.sync.dma_start(out_v[:, :, at : at + cols], result[:])

        dealt_rows = deal_scales()
        gather_scales([(0, 0, HALF), (1, 0, HALF), (2, 0, HALF + BLOCK)],
                      keep.tile([P, LISTS * HALF + BLOCK], U8, name="picked_head", align_bytes=64),
                      keep.tile([P, (LISTS * HALF + BLOCK) // 4], I32, name="moved_head", align_bytes=64))

        parts = {}
        acts, hs, ys, res_sb = {}, {}, {}, {}
        for step, (block, g) in enumerate(steps):
            words = gather_words(step)
            if step in scales_in:
                run = scales_in[step]
                tile = shared.tile([P, run[2]], U8, name="picked%d" % step, offset=zone[step - 1] + 4 * BLOCK, align_bytes=64)
                dst = shared.tile([P, run[2] // 4], I32, name="moved%d" % step,
                                  offset=raw_at[0] + 9 * N + run[0] * HALF + run[1] - HALF, align_bytes=64)
                gather_scales([run], tile, dst)
            if step == len(steps) - 1:
                for m in range(2):
                    ys[m] = second(m, quantise(m, hs[m]))
            parted = part(step, words)
            if step < LISTS:
                deal(step)
            if step == 0:
                late_planes = shared.tile([P, 2, R // 4], I32, name="late_planes", offset=raw_at[0] + 5 * N, align_bytes=64)
                for q in range(4):
                    nc.sync.dma_start(late_planes[32 * q : 32 * q + 4, :, :], dealt_rows[64 + 8 * q : 64 + 8 * q + 8, :])
                sm_sb = shared.tile([P, 4], F32, name="sm_sb", offset=raw_at[0] + LINK, align_bytes=64)
                nc.sync.dma_start(sm_sb[:], sm.rearrange("(p t) -> p t", t=4))
                wd_sb = shared.tile([P, 2 * N // 4], I32, name="wd_sb", offset=raw_at[0] + N, align_bytes=64)
                nc.sync.dma_start(wd_sb[:], wd_words[0].bitcast(I32))
                wd_plane = shared.tile([P, N // 4], I32, name="wd_plane", offset=raw_at[0] + 4 * N, align_bytes=64)
                for q in range(4):
                    nc.sync.dma_start(wd_plane[32 * q : 32 * q + 4, :], wd_scales.bitcast(I32)[0, 4 * q : 4 * q + 4, :])
            for n in pieces_of[block]:
                parts[step] = parted
                project(n, g, parted, (0,) if step < 2 else (0, 1))
                if step == 1:
                    for early in range(2):
                        project(0, early, parts[early], (1,))
                if g == LISTS - 1:
                    acts[n] = activate(n)
                    hs[n] = shared.tile([P, pieces[n][1], 4], BF16, name="h%d" % n, offset=h_at[n], align_bytes=64)
                    if n < BLOCKS - 2:
                        smooth_scalar(n, acts[n][:], hs[n][:])
                    elif n < BLOCKS - 1:
                        smooth_scalar(n, acts[n][:, :, 0:P], hs[n][:, 0:P, :])
                        smooth_vector(acts[n][:, :, P:BLOCK], hs[n][:, P:BLOCK, :], nc.gpsimd)
            if 3 <= step < 3 + BLOCKS:
                b = step - 3
                res_sb[b] = shared.tile([P, 2, BLOCK], F32, name="res%d" % b, offset=raw_at[1] + 8 * BLOCK * b, align_bytes=64)
                nc.sync.dma_start(res_sb[b][:], res_v[:, :, b * BLOCK : (b + 1) * BLOCK])
        ys[2] = second(2, quantise(2, hs[2]))
        for m in (3, 4):
            smooth_vector(acts[m][:], hs[m][:], nc.vector)
        for m in (3, 4):
            ys[m] = second(m, quantise(m, hs[m]))
        for m in range(len(pieces)):
            finish(m, ys[m])
